import numpy as np
import ml_dtypes


def mxq(x, axis, fmt="e4m3"):
    dtype, down = {"e4m3": (ml_dtypes.float8_e4m3fn, 7), "e5m2": (ml_dtypes.float8_e5m2, 14)}[fmt]
    v = np.moveaxis(np.asarray(x, np.float32).astype(ml_dtypes.bfloat16).astype(np.float64), axis, -1)
    blocks = v.reshape(v.shape[:-1] + (-1, 32))
    amax = np.abs(blocks).max(-1, keepdims=True)
    byte = np.maximum(np.where(amax > 0, np.frexp(amax)[1] - 1 + 127, 0) - down, 1)
    scale = np.exp2(byte - 127.0)
    codes = (blocks / scale).astype(np.float32).astype(dtype).astype(np.float64)
    return np.moveaxis((codes * scale).reshape(v.shape), -1, axis)


WIDE = False


def mx_kscale(k):
    if not WIDE:
        return np.ones(k)
    levels = np.array([10, -10, 5, -5, 0])
    if k % 512:
        return np.exp2(np.random.permutation(np.resize(levels, k // 32))).repeat(32)
    a = np.empty((k // 512, 16))
    for p in range(k // 512):
        a[p, :8] = np.random.permutation(np.resize(levels, 8))
        for g in range(8):
            far = levels[np.abs(levels - a[p, g]) >= 10]
            a[p, g + 8] = far[np.random.randint(len(far))]
    return np.exp2(a.ravel()).repeat(32)


def f64(x):
    return np.asarray(x).astype(np.float64)


def striped(idx):
    return np.tile(idx.reshape(-1, 16).T, (8, 1)).astype(np.uint16)


def unstriped(offs):
    return offs[:16].T.reshape(-1).astype(np.int64)


E2M1 = np.array([0.0, 0.5, 1.0, 1.5, 2.0, 3.0, 4.0, 6.0, -0.0, -0.5, -1.0, -1.5, -2.0, -3.0, -4.0, -6.0])


def pack_fp4(w):
    k, n = w.shape
    w = f64(np.asarray(w, np.float32).astype(ml_dtypes.bfloat16)).reshape(k // 32, 32, n)
    amax = np.abs(w).max(1)
    mant, ex = np.frexp(amax / 6.0)
    byte = np.clip(np.where(amax > 0, np.where(mant > 0.5, ex, ex - 1) + 127, 1), 1, 254)
    scaled = (w * np.exp2(127.0 - byte)[:, None, :]).reshape(k, n).astype(np.float32)
    c = np.ascontiguousarray(scaled.reshape(k // 512, 128, 4, n).transpose(0, 1, 3, 2)).astype(ml_dtypes.float4_e2m1fn).view(np.uint8) & 0xF
    words = (c[..., 0::2] | (c[..., 1::2] << 4)).reshape(k // 512, 128, 2 * n)
    return np.ascontiguousarray(words), np.ascontiguousarray(byte.astype(np.uint8).reshape(k // 512, 16, n))


def unpack_fp4(words, scales):
    g, _, n = scales.shape
    words = np.ascontiguousarray(words).reshape(g, 128, n, 2)
    nib = np.empty((g, 128, n, 4), np.uint8)
    nib[..., 0::2] = words & 0xF
    nib[..., 1::2] = words >> 4
    vals = E2M1[nib] * np.repeat(np.exp2(scales.astype(np.float64) - 127.0), 8, axis=1)[..., None]
    return vals.transpose(0, 1, 3, 2).reshape(g * 512, n)


def relu(v):
    return np.maximum(v, 0.0)


K, T, S, H, N = 512, 2048, 1024, 512, 256
P = 2 ** 7


def setup_inputs():
    n = np.random.standard_normal
    s = mx_kscale(K)[:, None]
    u = mx_kscale(H)
    packed_w2 = pack_fp4(n((H, N)) / np.sqrt(H) / u[:, None])
    return {
        "xT": (n((K, T)) * s).astype(np.float32),
        "w1": (n((K, H)) / np.sqrt(K) / s * u).astype(np.float32),
        "w2_words": packed_w2[0],
        "w2_scales": packed_w2[1],
        "share": np.tile(np.random.uniform(0.1, 0.9, S), (P, 1)).astype(np.float32),
        "offs": striped(np.random.permutation(T)[:S]),
        "par": striped(np.random.permutation(S)[(S * np.random.uniform(0, 1, S) ** 4).astype(np.int64)]),
    }


def reference(xT, w1, w2_words, w2_scales, share, offs, par):
    xq = mxq(f64(xT)[:, unstriped(offs)], 0, "e4m3")
    h = relu(mxq(f64(w1), 0, "e4m3").T @ xq)
    z = h + h[:, unstriped(par)] * f64(share)[:1]
    return unpack_fp4(w2_words, w2_scales).T @ mxq(z, 0, "e4m3")

@@ -1,0 +1,203 @@
+from contextlib import ExitStack
+
+import concourse.mybir as mybir
+
+K, T, S, H, N = 512, 2048, 1024, 512, 256
+P = 128
+FLOPS = 2 * K * H * S + 2 * H * N * S
+
+F32 = mybir.dt.float32
+BF16 = mybir.dt.bfloat16
+I32 = mybir.dt.int32
+U32 = mybir.dt.uint32
+U16 = mybir.dt.uint16
+U8 = mybir.dt.uint8
+FP8X4 = mybir.dt.float8_e4m3fn_x4
+FP4X4 = mybir.dt.float4_e2m1fn_x4
+ALU = mybir.AluOpType
+ACT = mybir.ActivationFunctionType
+
+X_LOADS = [(0, 0, 1024, 640), (0, 1024, 1024, 640), (1, 0, 1024, 768), (1, 1024, 512, 384), (1, 1536, 256, 256), (1, 1792, 256, 0)]
+X_CHUNKS = [(0, 512), (512, 256), (768, 256)]
+Z_CHUNKS = [(0, 256), (256, 256), (512, 256), (768, 128), (896, 128)]
+
+
+def tile_picked_treeup_relu_e_kernel(tc, xT, w1, w2_words, w2_scales, share, offs, par, out):
+    nc = tc.nc
+    with ExitStack() as ctx:
+        keep = ctx.enter_context(tc.tile_pool(name="keep", bufs=1))
+        psum_h = ctx.enter_context(tc.psum_pool(name="psum_h", bufs=4))
+        psum_o = ctx.enter_context(tc.psum_pool(name="psum_o", bufs=4))
+
+        offs_sb = keep.tile([P, S // 16], U16, name="offs_sb")
+        par_sb = keep.tile([P, S // 16], U16, name="par_sb")
+        w2_scale = keep.tile([P, N], U8, name="w2_scale", align_bytes=64)
+        nc.gpsimd.memset(w2_scale[:], 0)
+
+        x_rows = xT.rearrange("(p j) t -> p j t", j=4)
+        raws = []
+        for n, (u, c0, width,  rest) in enumerate(X_LOADS):
+            raw = keep.tile([P, 2, width], F32, name="raw%d" % n)
+            nc.sync.dma_start(out=raw[:], in_=x_rows[:, 2 * u : 2 * u + 2, c0 : c0 + width])
+            raws.append(raw)
+            if n == 0:
+                nc.sync.dma_start(offs_sb[:], offs)
+        w_raw = keep.tile([P, 4, H], F32, name="w_raw")
+        nc.sync.dma_start(out=w_raw[:], in_=w1.rearrange("(p j) c -> p j c", j=4))
+        share_sb = keep.tile([P, S], F32, name="share_sb")
+        nc.sync.dma_start(out=share_sb[:], in_=share)
+        nc.sync.dma_start(par_sb[:], par)
+        w2_code = keep.tile([P, 2 * N], U8, name="w2_code", align_bytes=64)
+        nc.sync.dma_start(out=w2_code[:].bitcast(I32), in_=w2_words[0].bitcast(I32))
+        for q in range(4):
+            nc.sync.dma_start(out=w2_scale[32 * q : 32 * q + 4, :].bitcast(I32), in_=w2_scales[0, 4 * q : 4 * q + 4, :].bitcast(I32))
+
+        pairs = [keep.tile([P, T, 2], BF16, name="pairs%d" % u, align_bytes=64) for u in range(2)]
+        picked = [keep.tile([P, n, 2], U32, name="picked%d" % c, align_bytes=64) for c, (s0, n) in enumerate(X_CHUNKS)]
+        x_code = [keep.tile([P, n], U32, name="x_code%d" % c, align_bytes=64) for c, (s0, n) in enumerate(X_CHUNKS)]
+        x_scale = [keep.tile([P, n], U8, name="x_scale%d" % c, align_bytes=64) for c, (s0, n) in enumerate(X_CHUNKS)]
+
+        def cast(engine_copy, n, a, b):
+            u, c0, width, rest = X_LOADS[n]
+            engine_copy(
+                out=pairs[u][:, c0 + a : c0 + b, :].rearrange("p (c i) j -> p c j i", i=4),
+                in_=raws[n][:, :, a:b].rearrange("p j (c i) -> p c j i", i=4),
+            )
+
+        def pick(u, c):
+            s0, n = X_CHUNKS[c]
+            window = pairs[u][:].rearrange("p t j -> p (t j)").bitcast(U32)
+            nc.vector.tensor_copy(out=picked[c][:, :, u], in_=window.indirect(offs_sb[:, s0 // 16 : (s0 + n) // 16]))
+
+        def quantise_x(c):
+            nc.vector.quantize_mx(
+                out=x_code[c][:].bitcast(FP8X4),
+                scales=x_scale[c][:],
+                in_=picked[c][:].rearrange("p n u -> p (n u)").bitcast(BF16),
+            )
+
+        for n, (u, c0, width, split) in enumerate(X_LOADS):
+            if split > 0:
+                cast(nc.scalar.copy, n, 0, split)
+            if split < width:
+                cast(nc.vector.tensor_copy, n, split, width)
+            if n == 1:
+                for c in range(len(X_CHUNKS)):
+                    pick(0, c)
+
+        w_group = [keep.tile([P, P, 4], BF16, name="w_group%d" % t, align_bytes=64) for t in range(4)]
+        w_code = [keep.tile([P, P], U32, name="w_code%d" % t, align_bytes=64) for t in range(4)]
+        w_scale = [keep.tile([P, P], U8, name="w_scale%d" % t, align_bytes=64) for t in range(4)]
+        w_cols = w_raw[:].rearrange("p j (m t) -> p t m j", t=4)
+
+        def group_w(t):
+            nc.scalar.copy(out=w_group[t][:], in_=w_cols[:, t, :, :])
+
+        def quantise_w(t):
+            nc.vector.quantize_mx(
+                out=w_code[t][:].bitcast(FP8X4), scales=w_scale[t][:], in_=w_group[t][:].rearrange("p m j -> p (m j)")
+            )
+
+        group_w(0)
+        group_w(1)
+        pick(1, 0)
+        pick(1, 1)
+        quantise_x(0)
+        pick(1, 2)
+        quantise_x(1)
+        quantise_w(0)
+        quantise_x(2)
+        quantise_w(1)
+
+        h = [keep.tile([P, S], F32, name="h%d" % t) for t in range(4)]
+        h_all = keep.tile([P, 4, S], F32, name="h_all")
+
+        def layer1(t):
+            for half in range(2):
+                bank = psum_h.tile([P, 512], F32, name="bank")
+                for c, (s0, n) in enumerate(X_CHUNKS):
+                    if s0 // 512 != half:
+                        continue
+                    cols = slice(s0 % 512, s0 % 512 + n)
+                    nc.tensor.matmul_mx(
+                        out=bank[:, cols],
+                        lhsT=w_code[t][:].bitcast(FP8X4),
+                        lhsT_scale=w_scale[t][:],
+                        rhs=x_code[c][:].bitcast(FP8X4),
+                        rhs_scale=x_scale[c][:],
+                        start=True,
+                        stop=True,
+                    )
+                nc.scalar.activation(out=h[t][:, 512 * half : 512 * half + 512], in_=bank[:], func=ACT.Relu)
+            nc.sync.dma_start(out=h_all[:, t, :], in_=h[t][:])
+
+        taken = [keep.tile([P, 4, n], F32, name="taken%d" % c) for c, (s0, n) in enumerate(Z_CHUNKS)]
+        z = [keep.tile([P, n, 4], BF16, name="z%d" % c, align_bytes=64) for c, (s0, n) in enumerate(Z_CHUNKS)]
+        z_code = [keep.tile([P, n], U32, name="z_code%d" % c, align_bytes=64) for c, (s0, n) in enumerate(Z_CHUNKS)]
+        z_scale = [keep.tile([P, n], U8, name="z_scale%d" % c, align_bytes=64) for c, (s0, n) in enumerate(Z_CHUNKS)]
+
+        def follow(t, c):
+            s0, n = Z_CHUNKS[c]
+            nc.vector.tensor_tensor(
+                out=taken[c][:, t, :],
+                in0=h[t][:].indirect(par_sb[:, s0 // 16 : (s0 + n) // 16]),
+                in1=share_sb[:, s0 : s0 + n],
+                op=ALU.mult,
+            )
+
+        def add(c):
+            s0, n = Z_CHUNKS[c]
+            nc.vector.tensor_tensor(
+                out=z[c][:].rearrange("p (c i) t -> p c t i", i=4),
+                in0=taken[c][:].rearrange("p t (c i) -> p c t i", i=4),
+                in1=h_all[:, :, s0 : s0 + n].rearrange("p t (c i) -> p c t i", i=4),
+                op=ALU.add,
+            )
+
+        def layer2(c):
+            s0, n = Z_CHUNKS[c]
+            nc.vector.quantize_mx(
+                out=z_code[c][:].bitcast(FP8X4), scales=z_scale[c][:], in_=z[c][:].rearrange("p n t -> p (n t)")
+            )
+            for m in range(2):
+                bank = psum_o.tile([P, n], F32, name="obank")
+                nc.tensor.matmul_mx(
+                    out=bank[:],
+                    lhsT=w2_code[:, 2 * P * m : 2 * P * (m + 1)].bitcast(FP4X4),
+                    lhsT_scale=w2_scale[:, P * m : P * (m + 1)],
+                    rhs=z_code[c][:].bitcast(FP8X4),
+                    rhs_scale=z_scale[c][:],
+                    start=True,
+                    stop=True,
+                )
+                res = keep.tile([P, n], F32, name="res%d_%d" % (c, m))
+                if c == len(Z_CHUNKS) - 1 and m == 1:
+                    nc.vector.tensor_copy(out=res[:], in_=bank[:])
+                else:
+                    nc.scalar.copy(out=res[:], in_=bank[:])
+                nc.sync.dma_start(out=out[P * m : P * (m + 1), s0 : s0 + n], in_=res[:])
+
+        layer1(0)
+        group_w(2)
+        layer1(1)
+        group_w(3)
+        chunks = range(len(Z_CHUNKS))
+        for c in chunks:
+            follow(0, c)
+            if c == 0:
+                quantise_w(2)
+            if c == 2:
+                quantise_w(3)
+                layer1(2)
+                layer1(3)
+        for t in (1, 2):
+            for c in chunks:
+                follow(t, c)
+        follow(3, 0)
+        for c in chunks:
+            if c + 1 < len(Z_CHUNKS):
+                follow(3, c + 1)
+            add(c)
+            if c > 0:
+                layer2(c - 1)
+        layer2(len(Z_CHUNKS) - 1)

@@ -1,6 +1,7 @@
 from contextlib import ExitStack
 
 import concourse.mybir as mybir
+from concourse.masks import make_identity
 
 K, T, S, H, N = 512, 2048, 1024, 512, 256
 P = 128
@@ -17,26 +18,31 @@ FP4X4 = mybir.dt.float4_e2m1fn_x4
 ALU = mybir.AluOpType
 ACT = mybir.ActivationFunctionType
 
-X_LOADS = [(0, 0, 1024, 640), (0, 1024, 1024, 640), (1, 0, 1024, 768), (1, 1024, 512, 384), (1, 1536, 256, 256), (1, 1792, 256, 0)]
-X_CHUNKS = [(0, 512), (512, 256), (768, 256)]
-Z_CHUNKS = [(0, 256), (256, 256), (512, 256), (768, 128), (896, 128)]
+X_LOADS = [(0, 0, 1024, 768), (0, 1024, 1024, 384), (1, 0, 1024, 640), (1, 1024, 512, 256), (1, 1536, 256, 0), (1, 1792, 256, 0)]
+X_CHUNKS = [(0, 512), (512, 256), (768, 128), (896, 128)]
+PE_CHUNKS = [(0, 256), (256, 256), (512, 256)]
+V_CHUNKS = [(768, 128), (896, 128)]
+Z_CHUNKS = PE_CHUNKS + V_CHUNKS
+V0 = V_CHUNKS[0][0]
 
 
 def tile_picked_treeup_relu_e_kernel(tc, xT, w1, w2_words, w2_scales, share, offs, par, out):
     nc = tc.nc
     with ExitStack() as ctx:
         keep = ctx.enter_context(tc.tile_pool(name="keep", bufs=1))
-        psum_h = ctx.enter_context(tc.psum_pool(name="psum_h", bufs=4))
-        psum_o = ctx.enter_context(tc.psum_pool(name="psum_o", bufs=4))
+        psum_h = ctx.enter_context(tc.psum_pool(name="psum_h", bufs=5))
+        psum_f = ctx.enter_context(tc.psum_pool(name="psum_f", bufs=3))
 
         offs_sb = keep.tile([P, S // 16], U16, name="offs_sb")
         par_sb = keep.tile([P, S // 16], U16, name="par_sb")
         w2_scale = keep.tile([P, N], U8, name="w2_scale", align_bytes=64)
         nc.gpsimd.memset(w2_scale[:], 0)
+        ident = keep.tile([P, P], F32, name="ident")
+        make_identity(nc, ident[:])
 
         x_rows = xT.rearrange("(p j) t -> p j t", j=4)
         raws = []
-        for n, (u, c0, width,  rest) in enumerate(X_LOADS):
+        for n, (u, c0, width, split) in enumerate(X_LOADS):
             raw = keep.tile([P, 2, width], F32, name="raw%d" % n)
             nc.sync.dma_start(out=raw[:], in_=x_rows[:, 2 * u : 2 * u + 2, c0 : c0 + width])
             raws.append(raw)
@@ -44,8 +50,10 @@ def tile_picked_treeup_relu_e_kernel(tc, xT, w1, w2_words, w2_scales, share, off
                 nc.sync.dma_start(offs_sb[:], offs)
         w_raw = keep.tile([P, 4, H], F32, name="w_raw")
         nc.sync.dma_start(out=w_raw[:], in_=w1.rearrange("(p j) c -> p j c", j=4))
-        share_sb = keep.tile([P, S], F32, name="share_sb")
-        nc.sync.dma_start(out=share_sb[:], in_=share)
+        share_sb = {}
+        for s0, n in [(0, V0), (V0, S - V0)]:
+            share_sb.setdefault(s0, keep.tile([P, n], F32, name="share%d" % s0, tag="share%d" % s0, align_bytes=64))
+            nc.sync.dma_start(out=share_sb[s0][:], in_=share[:, s0 : s0 + n])
         nc.sync.dma_start(par_sb[:], par)
         w2_code = keep.tile([P, 2 * N], U8, name="w2_code", align_bytes=64)
         nc.sync.dma_start(out=w2_code[:].bitcast(I32), in_=w2_words[0].bitcast(I32))
@@ -53,27 +61,42 @@ def tile_picked_treeup_relu_e_kernel(tc, xT, w1, w2_words, w2_scales, share, off
             nc.sync.dma_start(out=w2_scale[32 * q : 32 * q + 4, :].bitcast(I32), in_=w2_scales[0, 4 * q : 4 * q + 4, :].bitcast(I32))
 
         pairs = [keep.tile([P, T, 2], BF16, name="pairs%d" % u, align_bytes=64) for u in range(2)]
-        picked = [keep.tile([P, n, 2], U32, name="picked%d" % c, align_bytes=64) for c, (s0, n) in enumerate(X_CHUNKS)]
-        x_code = [keep.tile([P, n], U32, name="x_code%d" % c, align_bytes=64) for c, (s0, n) in enumerate(X_CHUNKS)]
+        got = keep.tile([P, 2, S], U32, name="got")
+        picked = {}
         x_scale = [keep.tile([P, n], U8, name="x_scale%d" % c, align_bytes=64) for c, (s0, n) in enumerate(X_CHUNKS)]
 
         def cast(engine_copy, n, a, b):
-            u, c0, width, rest = X_LOADS[n]
+            u, c0, width, split = X_LOADS[n]
             engine_copy(
-                out=pairs[u][:, c0 + a : c0 + b, :].rearrange("p (c i) j -> p c j i", i=4),
-                in_=raws[n][:, :, a:b].rearrange("p j (c i) -> p c j i", i=4),
+                out=pairs[u][:, c0 + a : c0 + b, :],
+                in_=raws[n][:, :, a:b].rearrange("p j c -> p c j"),
             )
 
-        def pick(u, c):
-            s0, n = X_CHUNKS[c]
+        def pick(u, s0, n):
             window = pairs[u][:].rearrange("p t j -> p (t j)").bitcast(U32)
-            nc.vector.tensor_copy(out=picked[c][:, :, u], in_=window.indirect(offs_sb[:, s0 // 16 : (s0 + n) // 16]))
+            nc.vector.tensor_copy(out=got[:, u, s0 : s0 + n], in_=window.indirect(offs_sb[:, s0 // 16 : (s0 + n) // 16]))
+
+        def weave(s0, n):
+            half = s0 // 512
+            if s0 % 512 == 0:
+                picked.setdefault(half, keep.tile([P, 512, 2], U32, name="picked%d" % half, tag="picked", align_bytes=64))
+            dst = picked[half][:, s0 % 512 : s0 % 512 + n, :]
+            src = got[:, :, s0 : s0 + n].rearrange("p u n -> p n u")
+            if half == 0:
+                nc.scalar.copy(out=dst, in_=src)
+            else:
+                nc.vector.tensor_copy(out=dst.bitcast(I32), in_=got[:].bitcast(I32)[:, :, s0 : s0 + n].rearrange("p u n -> p n u"))
+
+        x_code = {}
 
         def quantise_x(c):
+            s0, n = X_CHUNKS[c]
+            tag = "w_group0" if c == 1 else "x_code%d" % c
+            x_code.setdefault(c, keep.tile([P, n], U32, name="x_code%d" % c, tag=tag, align_bytes=64))
             nc.vector.quantize_mx(
                 out=x_code[c][:].bitcast(FP8X4),
                 scales=x_scale[c][:],
-                in_=picked[c][:].rearrange("p n u -> p (n u)").bitcast(BF16),
+                in_=picked[s0 // 512][:, s0 % 512 : s0 % 512 + n, :].rearrange("p n u -> p (n u)").bitcast(BF16),
             )
 
         for n, (u, c0, width, split) in enumerate(X_LOADS):
@@ -82,75 +105,131 @@ def tile_picked_treeup_relu_e_kernel(tc, xT, w1, w2_words, w2_scales, share, off
             if split < width:
                 cast(nc.vector.tensor_copy, n, split, width)
             if n == 1:
-                for c in range(len(X_CHUNKS)):
-                    pick(0, c)
+                pick(0, 0, S)
 
-        w_group = [keep.tile([P, P, 4], BF16, name="w_group%d" % t, align_bytes=64) for t in range(4)]
-        w_code = [keep.tile([P, P], U32, name="w_code%d" % t, align_bytes=64) for t in range(4)]
-        w_scale = [keep.tile([P, P], U8, name="w_scale%d" % t, align_bytes=64) for t in range(4)]
-        w_cols = w_raw[:].rearrange("p j (m t) -> p t m j", t=4)
+        w_group = [keep.tile([P, 2, P, 4], BF16, name="w_group%d" % u, tag="w_group%d" % u, align_bytes=64) for u in range(2)]
+        w_code = [keep.tile([P, 2 * P], U32, name="w_code%d" % u, align_bytes=64) for u in range(2)]
+        w_scale = [keep.tile([P, 2 * P], U8, name="w_scale%d" % u, align_bytes=64) for u in range(2)]
+        w_cols = w_raw[:].rearrange("p j (m t) -> p m t j", t=4)
 
-        def group_w(t):
-            nc.scalar.copy(out=w_group[t][:], in_=w_cols[:, t, :, :])
+        def group_w(u):
+            nc.scalar.copy(out=w_group[u][:].rearrange("p e m j -> p m e j"), in_=w_cols[:, :, 2 * u : 2 * u + 2, :])
 
-        def quantise_w(t):
+        def quantise_w(u):
             nc.vector.quantize_mx(
-                out=w_code[t][:].bitcast(FP8X4), scales=w_scale[t][:], in_=w_group[t][:].rearrange("p m j -> p (m j)")
+                out=w_code[u][:].bitcast(FP8X4), scales=w_scale[u][:], in_=w_group[u][:].rearrange("p e m j -> p (e m j)")
             )
 
+        pick(1, 0, 256)
+        weave(0, 256)
+        pick(1, 256, 256)
+        weave(256, 256)
+        pick(1, 512, 512)
         group_w(0)
         group_w(1)
-        pick(1, 0)
-        pick(1, 1)
         quantise_x(0)
-        pick(1, 2)
-        quantise_x(1)
+        weave(512, 512)
         quantise_w(0)
+        quantise_x(1)
         quantise_x(2)
+        quantise_x(3)
         quantise_w(1)
 
         h = [keep.tile([P, S], F32, name="h%d" % t) for t in range(4)]
-        h_all = keep.tile([P, 4, S], F32, name="h_all")
+        h_tail = keep.tile([P, 4, S - V0], F32, name="h_tail")
 
         def layer1(t):
-            for half in range(2):
-                bank = psum_h.tile([P, 512], F32, name="bank")
-                for c, (s0, n) in enumerate(X_CHUNKS):
-                    if s0 // 512 != half:
-                        continue
-                    cols = slice(s0 % 512, s0 % 512 + n)
+            w_cols_t = slice(P * (t % 2), P * (t % 2 + 1))
+            groups = [[0], [1], [2], [3]] if t == 0 else [[0], [1, 2, 3]]
+            for group in groups:
+                bank = psum_h.tile([P, 512], F32, name="bank", tag="mx")
+                first = X_CHUNKS[group[0]][0]
+                for c in group:
+                    s0, n = X_CHUNKS[c]
                     nc.tensor.matmul_mx(
-                        out=bank[:, cols],
-                        lhsT=w_code[t][:].bitcast(FP8X4),
-                        lhsT_scale=w_scale[t][:],
+                        out=bank[:, s0 - first : s0 - first + n],
+                        lhsT=w_code[t // 2][:, w_cols_t].bitcast(FP8X4),
+                        lhsT_scale=w_scale[t // 2][:, w_cols_t],
                         rhs=x_code[c][:].bitcast(FP8X4),
                         rhs_scale=x_scale[c][:],
                         start=True,
                         stop=True,
                     )
-                nc.scalar.activation(out=h[t][:, 512 * half : 512 * half + 512], in_=bank[:], func=ACT.Relu)
-            nc.sync.dma_start(out=h_all[:, t, :], in_=h[t][:])
+                width = s0 + n - first
+                if group[0] >= 2:
+                    nc.vector.tensor_scalar_max(h[t][:, first : first + width], bank[:, 0:width], 0.0)
+                else:
+                    nc.scalar.activation(out=h[t][:, first : first + width], in_=bank[:, 0:width], func=ACT.Relu)
+            nc.sync.dma_start(out=h_tail[:, t, :], in_=h[t][:, V0:S])
 
-        taken = [keep.tile([P, 4, n], F32, name="taken%d" % c) for c, (s0, n) in enumerate(Z_CHUNKS)]
-        z = [keep.tile([P, n, 4], BF16, name="z%d" % c, align_bytes=64) for c, (s0, n) in enumerate(Z_CHUNKS)]
+        taken = [keep.tile([P, V0], F32, name="taken%d" % t) for t in range(4)]
+        turned = [[keep.tile([P, n // P, P, 2], BF16, name="turned%d_%d" % (c, u)) for u in range(2)] for c, (s0, n) in enumerate(PE_CHUNKS)]
+        z = {}
+        taken_v = {}
+
+        def new_z(c):
+            tag = "z%d" % {3: 0, 4: 2}.get(c, c)
+            z.setdefault(c, keep.tile([P, Z_CHUNKS[c][1], 4], BF16, name="z%d" % c, tag=tag, align_bytes=64))
+
+        def new_taken_v(c):
+            tag = {3: "share0", 4: "z1"}[c]
+            taken_v.setdefault(c, keep.tile([P, 4, Z_CHUNKS[c][1]], F32, name="taken_v%d" % c, tag=tag, align_bytes=64))
+
         z_code = [keep.tile([P, n], U32, name="z_code%d" % c, align_bytes=64) for c, (s0, n) in enumerate(Z_CHUNKS)]
         z_scale = [keep.tile([P, n], U8, name="z_scale%d" % c, align_bytes=64) for c, (s0, n) in enumerate(Z_CHUNKS)]
 
-        def follow(t, c):
-            s0, n = Z_CHUNKS[c]
+        def follow(t, s0, n):
+            base = max(b for b in share_sb if b <= s0)
+            dst = taken[t][:, s0 : s0 + n] if s0 < V0 else taken_v[Z_CHUNKS.index((s0, n))][:, t, :]
             nc.vector.tensor_tensor(
-                out=taken[c][:, t, :],
+                out=dst,
                 in0=h[t][:].indirect(par_sb[:, s0 // 16 : (s0 + n) // 16]),
-                in1=share_sb[:, s0 : s0 + n],
+                in1=share_sb[base][:, s0 - base : s0 - base + n],
                 op=ALU.mult,
             )
 
+        sums = {}
+
+        def turn(name, t, c):
+            source = h if name == "h" else taken
+            s0, n = PE_CHUNKS[c]
+            u, e = divmod(t, 2)
+            first = name == "h" and e == 0
+            last = name == "taken" and e == 1
+            if first:
+                pool, tag = (psum_f, "turn") if u == 0 else (psum_h, "mx")
+                sums.setdefault((u, c), pool.tile([P, n // P, 2, P], F32, name="fbank", tag=tag))
+            bank = sums[(u, c)]
+            for b in range(n // P):
+                nc.tensor.matmul(
+                    bank[:, b, e, :],
+                    lhsT=source[t][:, s0 + P * b : s0 + P * (b + 1)],
+                    rhs=ident[:],
+                    is_transpose=True,
+                    start=first and b == 0,
+                    stop=last and b == n // P - 1,
+                )
+            if last:
+                nc.scalar.copy(out=turned[c][u][:], in_=bank[:].rearrange("s b e p -> s b p e"))
+
+        def turn_back(c):
+            s0, n = PE_CHUNKS[c]
+            bank = psum_f.tile([P, n // P, 2, P], F32, name="bbank", tag="turn")
+            for b in range(n // P):
+                for u in range(2):
+                    words = turned[c][u][:, b, :, :].rearrange("s p e -> s (p e)").bitcast(F32)
+                    nc.tensor.transpose(bank[:, b, u, :], words, ident[:])
+            new_z(c)
+            z_words = z[c][:].rearrange("p n t -> p (n t)").bitcast(F32).rearrange("p (b s u) -> p b s u", u=2, s=P)
+            nc.scalar.copy(out=z_words, in_=bank[:].rearrange("p b u s -> p b s u"))
+
         def add(c):
+            new_z(c)
             s0, n = Z_CHUNKS[c]
             nc.vector.tensor_tensor(
                 out=z[c][:].rearrange("p (c i) t -> p c t i", i=4),
-                in0=taken[c][:].rearrange("p t (c i) -> p c t i", i=4),
-                in1=h_all[:, :, s0 : s0 + n].rearrange("p t (c i) -> p c t i", i=4),
+                in0=taken_v[c][:].rearrange("p t (c i) -> p c t i", i=4),
+                in1=h_tail[:, :, s0 - V0 : s0 - V0 + n].rearrange("p t (c i) -> p c t i", i=4),
                 op=ALU.add,
             )
 
@@ -159,45 +238,56 @@ def tile_picked_treeup_relu_e_kernel(tc, xT, w1, w2_words, w2_scales, share, off
             nc.vector.quantize_mx(
                 out=z_code[c][:].bitcast(FP8X4), scales=z_scale[c][:], in_=z[c][:].rearrange("p n t -> p (n t)")
             )
-            for m in range(2):
-                bank = psum_o.tile([P, n], F32, name="obank")
-                nc.tensor.matmul_mx(
-                    out=bank[:],
-                    lhsT=w2_code[:, 2 * P * m : 2 * P * (m + 1)].bitcast(FP4X4),
-                    lhsT_scale=w2_scale[:, P * m : P * (m + 1)],
-                    rhs=z_code[c][:].bitcast(FP8X4),
-                    rhs_scale=z_scale[c][:],
-                    start=True,
-                    stop=True,
-                )
-                res = keep.tile([P, n], F32, name="res%d_%d" % (c, m))
-                if c == len(Z_CHUNKS) - 1 and m == 1:
+            groups = [[0], [1]] if c == len(Z_CHUNKS) - 1 else [[0, 1]]
+            for group in groups:
+                bank = psum_h.tile([P, len(group), n], F32, name="obank", tag="mx")
+                for m in group:
+                    nc.tensor.matmul_mx(
+                        out=bank[:, m - group[0], :],
+                        lhsT=w2_code[:, 2 * P * m : 2 * P * (m + 1)].bitcast(FP4X4),
+                        lhsT_scale=w2_scale[:, P * m : P * (m + 1)],
+                        rhs=z_code[c][:].bitcast(FP8X4),
+                        rhs_scale=z_scale[c][:],
+                        start=True,
+                        stop=True,
+                    )
+                res = keep.tile([P, len(group), n], F32, name="res%d_%d" % (c, group[0]))
+                dst = out.rearrange("(m p) s -> p m s", p=P)[:, group[0] : group[-1] + 1, s0 : s0 + n]
+                if group == [1]:
                     nc.vector.tensor_copy(out=res[:], in_=bank[:])
                 else:
                     nc.scalar.copy(out=res[:], in_=bank[:])
-                nc.sync.dma_start(out=out[P * m : P * (m + 1), s0 : s0 + n], in_=res[:])
+                if group == [0]:
+                    nc.scalar.dma_start(out=dst, in_=res[:])
+                else:
+                    nc.sync.dma_start(out=dst, in_=res[:])
 
-        layer1(0)
-        group_w(2)
-        layer1(1)
-        group_w(3)
-        chunks = range(len(Z_CHUNKS))
-        for c in chunks:
-            follow(0, c)
-            if c == 0:
-                quantise_w(2)
-            if c == 2:
-                quantise_w(3)
-                layer1(2)
-                layer1(3)
-        for t in (1, 2):
-            for c in chunks:
-                follow(t, c)
-        follow(3, 0)
-        for c in chunks:
-            if c + 1 < len(Z_CHUNKS):
-                follow(3, c + 1)
-            add(c)
-            if c > 0:
-                layer2(c - 1)
-        layer2(len(Z_CHUNKS) - 1)
+        for t in range(4):
+            layer1(t)
+        pe = range(len(PE_CHUNKS))
+        for t in range(3):
+            follow(t, 0, V0)
+        for c in pe:
+            follow(3, 256 * c, 256)
+        for name, t in (("h", 0), ("h", 1), ("taken", 0), ("h", 2), ("taken", 1), ("h", 3), ("taken", 2)):
+            for c in pe:
+                turn(name, t, c)
+        turn("taken", 3, 0)
+        turn("taken", 3, 1)
+        turn_back(0)
+        turn("taken", 3, 2)
+        turn_back(1)
+        turn_back(2)
+        new_taken_v(3)
+        for t in range(4):
+            follow(t, 768, 128)
+        layer2(0)
+        add(3)
+        layer2(1)
+        new_taken_v(4)
+        for t in range(4):
+            follow(t, 896, 128)
+        layer2(3)
+        layer2(2)
+        add(4)
+        layer2(4)

@@ -18,10 +18,10 @@ FP4X4 = mybir.dt.float4_e2m1fn_x4
 ALU = mybir.AluOpType
 ACT = mybir.ActivationFunctionType
 
-X_LOADS = [(0, 0, 1024, 768), (0, 1024, 1024, 384), (1, 0, 1024, 640), (1, 1024, 512, 256), (1, 1536, 256, 0), (1, 1792, 256, 0)]
+X_LOADS = [(0, 0, 1024, 768), (0, 1024, 1024, 384), (1, 0, 1024, 640), (1, 1024, 512, 256), (1, 1536, 512, 192)]
 X_CHUNKS = [(0, 512), (512, 256), (768, 128), (896, 128)]
-PE_CHUNKS = [(0, 256), (256, 256), (512, 256)]
-V_CHUNKS = [(768, 128), (896, 128)]
+PE_CHUNKS = [(0, 256), (256, 256)]
+V_CHUNKS = [(512, 256), (768, 128), (896, 128)]
 Z_CHUNKS = PE_CHUNKS + V_CHUNKS
 V0 = V_CHUNKS[0][0]
 
@@ -30,8 +30,8 @@ def tile_picked_treeup_relu_e_kernel(tc, xT, w1, w2_words, w2_scales, share, off
     nc = tc.nc
     with ExitStack() as ctx:
         keep = ctx.enter_context(tc.tile_pool(name="keep", bufs=1))
-        psum_h = ctx.enter_context(tc.psum_pool(name="psum_h", bufs=5))
-        psum_f = ctx.enter_context(tc.psum_pool(name="psum_f", bufs=3))
+        psum_h = ctx.enter_context(tc.psum_pool(name="psum_h", bufs=6))
+        psum_f = ctx.enter_context(tc.psum_pool(name="psum_f", bufs=2))
 
         offs_sb = keep.tile([P, S // 16], U16, name="offs_sb")
         par_sb = keep.tile([P, S // 16], U16, name="par_sb")
@@ -51,7 +51,7 @@ def tile_picked_treeup_relu_e_kernel(tc, xT, w1, w2_words, w2_scales, share, off
         w_raw = keep.tile([P, 4, H], F32, name="w_raw")
         nc.sync.dma_start(out=w_raw[:], in_=w1.rearrange("(p j) c -> p j c", j=4))
         share_sb = {}
-        for s0, n in [(0, V0), (V0, S - V0)]:
+        for s0, n in Z_CHUNKS[0:3] + [(768, 256)]:
             share_sb.setdefault(s0, keep.tile([P, n], F32, name="share%d" % s0, tag="share%d" % s0, align_bytes=64))
             nc.sync.dma_start(out=share_sb[s0][:], in_=share[:, s0 : s0 + n])
         nc.sync.dma_start(par_sb[:], par)
@@ -163,24 +163,24 @@ def tile_picked_treeup_relu_e_kernel(tc, xT, w1, w2_words, w2_scales, share, off
             nc.sync.dma_start(out=h_tail[:, t, :], in_=h[t][:, V0:S])
 
         taken = [keep.tile([P, V0], F32, name="taken%d" % t) for t in range(4)]
-        turned = [[keep.tile([P, n // P, P, 2], BF16, name="turned%d_%d" % (c, u)) for u in range(2)] for c, (s0, n) in enumerate(PE_CHUNKS)]
+        turned = [[keep.tile([P, n // P, P, 2], BF16, name="turned%d_%d" % (c, u), tag="turned%d_%d" % (c, u), align_bytes=64) for u in range(2)] for c, (s0, n) in enumerate(PE_CHUNKS)]
         z = {}
         taken_v = {}
 
         def new_z(c):
-            tag = "z%d" % {3: 0, 4: 2}.get(c, c)
+            tag = "turned1_1" if c == 2 else "z%d" % c
             z.setdefault(c, keep.tile([P, Z_CHUNKS[c][1], 4], BF16, name="z%d" % c, tag=tag, align_bytes=64))
 
-        def new_taken_v(c):
-            tag = {3: "share0", 4: "z1"}[c]
-            taken_v.setdefault(c, keep.tile([P, 4, Z_CHUNKS[c][1]], F32, name="taken_v%d" % c, tag=tag, align_bytes=64))
+        def new_taken_v(c, u):
+            tag = {(2, 1): "share256", (3, 0): "share512", (3, 1): "taken_v2_0", (4, 0): "z1", (4, 1): "share512"}.get((c, u), "taken_v%d_%d" % (c, u))
+            taken_v.setdefault((c, u), keep.tile([P, 2, Z_CHUNKS[c][1]], F32, name="taken_v%d_%d" % (c, u), tag=tag, align_bytes=64))
 
         z_code = [keep.tile([P, n], U32, name="z_code%d" % c, align_bytes=64) for c, (s0, n) in enumerate(Z_CHUNKS)]
         z_scale = [keep.tile([P, n], U8, name="z_scale%d" % c, align_bytes=64) for c, (s0, n) in enumerate(Z_CHUNKS)]
 
         def follow(t, s0, n):
             base = max(b for b in share_sb if b <= s0)
-            dst = taken[t][:, s0 : s0 + n] if s0 < V0 else taken_v[Z_CHUNKS.index((s0, n))][:, t, :]
+            dst = taken[t][:, s0 : s0 + n] if s0 < V0 else taken_v[(Z_CHUNKS.index((s0, n)), t // 2)][:, t % 2, :]
             nc.vector.tensor_tensor(
                 out=dst,
                 in0=h[t][:].indirect(par_sb[:, s0 // 16 : (s0 + n) // 16]),
@@ -223,15 +223,30 @@ def tile_picked_treeup_relu_e_kernel(tc, xT, w1, w2_words, w2_scales, share, off
             z_words = z[c][:].rearrange("p n t -> p (n t)").bitcast(F32).rearrange("p (b s u) -> p b s u", u=2, s=P)
             nc.scalar.copy(out=z_words, in_=bank[:].rearrange("p b u s -> p b s u"))
 
-        def add(c):
-            new_z(c)
+        z_pairs = {}
+
+        def add(c, u):
             s0, n = Z_CHUNKS[c]
+            if u == 0:
+                tag = {2: "share0", 3: "z0", 4: "z_pairs"}[c]
+                z_pairs.setdefault(c, keep.tile([P, 2, n, 2], BF16, name="z_pairs%d" % c, tag=tag, align_bytes=64))
             nc.vector.tensor_tensor(
-                out=z[c][:].rearrange("p (c i) t -> p c t i", i=4),
-                in0=taken_v[c][:].rearrange("p t (c i) -> p c t i", i=4),
-                in1=h_tail[:, :, s0 - V0 : s0 - V0 + n].rearrange("p t (c i) -> p c t i", i=4),
+                out=z_pairs[c][:, u, :, :],
+                in0=taken_v[(c, u)][:].rearrange("p e n -> p n e"),
+                in1=h_tail[:, 2 * u : 2 * u + 2, s0 - V0 : s0 - V0 + n].rearrange("p e n -> p n e"),
                 op=ALU.add,
             )
+
+        def weave_z(c):
+            new_z(c)
+            last = c == len(Z_CHUNKS) - 1
+            word = I32 if last else U32
+            dst = z[c][:].rearrange("p n t -> p (n t)").bitcast(word).rearrange("p (n u) -> p n u", u=2)
+            src = z_pairs[c][:].rearrange("p u n e -> p (u n e)").bitcast(word).rearrange("p (u n) -> p n u", u=2)
+            if last:
+                nc.vector.tensor_copy(out=dst, in_=src)
+            else:
+                nc.scalar.copy(out=dst, in_=src)
 
         def layer2(c):
             s0, n = Z_CHUNKS[c]
@@ -265,29 +280,39 @@ def tile_picked_treeup_relu_e_kernel(tc, xT, w1, w2_words, w2_scales, share, off
         for t in range(4):
             layer1(t)
         pe = range(len(PE_CHUNKS))
-        for t in range(3):
-            follow(t, 0, V0)
-        for c in pe:
-            follow(3, 256 * c, 256)
-        for name, t in (("h", 0), ("h", 1), ("taken", 0), ("h", 2), ("taken", 1), ("h", 3), ("taken", 2)):
+        new_taken_v(2, 0)
+        for t in range(4):
+            for c in pe:
+                follow(t, 256 * c, 256)
+            if t < 2:
+                follow(t, 512, 256)
+        for name, t in (("h", 0), ("h", 1), ("taken", 0), ("h", 2), ("taken", 1), ("h", 3), ("taken", 2), ("taken", 3)):
             for c in pe:
                 turn(name, t, c)
-        turn("taken", 3, 0)
-        turn("taken", 3, 1)
-        turn_back(0)
-        turn("taken", 3, 2)
-        turn_back(1)
-        turn_back(2)
-        new_taken_v(3)
+        for c in pe:
+            turn_back(c)
+        new_taken_v(2, 1)
+        follow(2, 512, 256)
+        follow(3, 512, 256)
+        add(2, 0)
+        add(2, 1)
+        weave_z(2)
         for t in range(4):
+            if t % 2 == 0:
+                new_taken_v(3, t // 2)
             follow(t, 768, 128)
         layer2(0)
-        add(3)
+        add(3, 0)
+        add(3, 1)
+        weave_z(3)
         layer2(1)
-        new_taken_v(4)
         for t in range(4):
+            if t % 2 == 0:
+                new_taken_v(4, t // 2)
             follow(t, 896, 128)
-        layer2(3)
         layer2(2)
-        add(4)
+        add(4, 0)
+        add(4, 1)
+        layer2(3)
+        weave_z(4)
         layer2(4)

@@ -1,7 +1,6 @@
 from contextlib import ExitStack
 
 import concourse.mybir as mybir
-from concourse.masks import make_identity
 
 K, T, S, H, N = 512, 2048, 1024, 512, 256
 P = 128
@@ -20,25 +19,20 @@ ACT = mybir.ActivationFunctionType
 
 X_LOADS = [(0, 0, 1024, 768), (0, 1024, 1024, 384), (1, 0, 1024, 640), (1, 1024, 512, 256), (1, 1536, 512, 192)]
 X_CHUNKS = [(0, 512), (512, 256), (768, 128), (896, 128)]
-PE_CHUNKS = [(0, 256), (256, 256)]
-V_CHUNKS = [(512, 256), (768, 128), (896, 128)]
-Z_CHUNKS = PE_CHUNKS + V_CHUNKS
-V0 = V_CHUNKS[0][0]
+Z_CHUNKS = [(0, 256), (256, 256), (512, 256), (768, 128), (896, 128)]
+LINE = 4
 
 
 def tile_picked_treeup_relu_e_kernel(tc, xT, w1, w2_words, w2_scales, share, offs, par, out):
     nc = tc.nc
     with ExitStack() as ctx:
         keep = ctx.enter_context(tc.tile_pool(name="keep", bufs=1))
-        psum_h = ctx.enter_context(tc.psum_pool(name="psum_h", bufs=6))
-        psum_f = ctx.enter_context(tc.psum_pool(name="psum_f", bufs=2))
+        psum = ctx.enter_context(tc.psum_pool(name="psum", bufs=8))
 
         offs_sb = keep.tile([P, S // 16], U16, name="offs_sb")
         par_sb = keep.tile([P, S // 16], U16, name="par_sb")
         w2_scale = keep.tile([P, N], U8, name="w2_scale", align_bytes=64)
         nc.gpsimd.memset(w2_scale[:], 0)
-        ident = keep.tile([P, P], F32, name="ident")
-        make_identity(nc, ident[:])
 
         x_rows = xT.rearrange("(p j) t -> p j t", j=4)
         raws = []
@@ -50,11 +44,9 @@ def tile_picked_treeup_relu_e_kernel(tc, xT, w1, w2_words, w2_scales, share, off
                 nc.sync.dma_start(offs_sb[:], offs)
         w_raw = keep.tile([P, 4, H], F32, name="w_raw")
         nc.sync.dma_start(out=w_raw[:], in_=w1.rearrange("(p j) c -> p j c", j=4))
-        share_sb = {}
-        for s0, n in Z_CHUNKS[0:3] + [(768, 256)]:
-            share_sb.setdefault(s0, keep.tile([P, n], F32, name="share%d" % s0, tag="share%d" % s0, align_bytes=64))
-            nc.sync.dma_start(out=share_sb[s0][:], in_=share[:, s0 : s0 + n])
         nc.sync.dma_start(par_sb[:], par)
+        share_sb = keep.tile([P, S], F32, name="share_sb")
+        nc.sync.dma_start(out=share_sb[:], in_=share)
         w2_code = keep.tile([P, 2 * N], U8, name="w2_code", align_bytes=64)
         nc.sync.dma_start(out=w2_code[:].bitcast(I32), in_=w2_words[0].bitcast(I32))
         for q in range(4):
@@ -62,32 +54,30 @@ def tile_picked_treeup_relu_e_kernel(tc, xT, w1, w2_words, w2_scales, share, off
 
         pairs = [keep.tile([P, T, 2], BF16, name="pairs%d" % u, align_bytes=64) for u in range(2)]
         got = keep.tile([P, 2, S], U32, name="got")
-        picked = {}
+        picked = [keep.tile([P, 512, 2], U32, name="picked%d" % half, align_bytes=64) for half in range(2)]
+        x_code = {}
         x_scale = [keep.tile([P, n], U8, name="x_scale%d" % c, align_bytes=64) for c, (s0, n) in enumerate(X_CHUNKS)]
 
         def cast(engine_copy, n, a, b):
             u, c0, width, split = X_LOADS[n]
             engine_copy(
-                out=pairs[u][:, c0 + a : c0 + b, :],
-                in_=raws[n][:, :, a:b].rearrange("p j c -> p c j"),
+                out=pairs[u][:, c0 + a : c0 + b, :].rearrange("p (c i) j -> p c j i", i=LINE),
+                in_=raws[n][:, :, a:b].rearrange("p j (c i) -> p c j i", i=LINE),
             )
 
         def pick(u, s0, n):
             window = pairs[u][:].rearrange("p t j -> p (t j)").bitcast(U32)
             nc.vector.tensor_copy(out=got[:, u, s0 : s0 + n], in_=window.indirect(offs_sb[:, s0 // 16 : (s0 + n) // 16]))
 
-        def weave(s0, n):
-            half = s0 // 512
-            if s0 % 512 == 0:
-                picked.setdefault(half, keep.tile([P, 512, 2], U32, name="picked%d" % half, tag="picked", align_bytes=64))
-            dst = picked[half][:, s0 % 512 : s0 % 512 + n, :]
-            src = got[:, :, s0 : s0 + n].rearrange("p u n -> p n u")
-            if half == 0:
+        def weave(c, a, n, on_scalar):
+            s0 = 512 * c + a
+            word = U32 if on_scalar else I32
+            dst = picked[c][:].bitcast(word)[:, a : a + n, :].rearrange("p (c i) u -> p c u i", i=LINE)
+            src = got[:].bitcast(word)[:, :, s0 : s0 + n].rearrange("p u (c i) -> p c u i", i=LINE)
+            if on_scalar:
                 nc.scalar.copy(out=dst, in_=src)
             else:
-                nc.vector.tensor_copy(out=dst.bitcast(I32), in_=got[:].bitcast(I32)[:, :, s0 : s0 + n].rearrange("p u n -> p n u"))
-
-        x_code = {}
+                nc.vector.tensor_copy(out=dst, in_=src)
 
         def quantise_x(c):
             s0, n = X_CHUNKS[c]
@@ -100,20 +90,18 @@ def tile_picked_treeup_relu_e_kernel(tc, xT, w1, w2_words, w2_scales, share, off
             )
 
         for n, (u, c0, width, split) in enumerate(X_LOADS):
-            if split > 0:
-                cast(nc.scalar.copy, n, 0, split)
-            if split < width:
-                cast(nc.vector.tensor_copy, n, split, width)
+            cast(nc.scalar.copy, n, 0, split)
+            cast(nc.vector.tensor_copy, n, split, width)
             if n == 1:
                 pick(0, 0, S)
 
         w_group = [keep.tile([P, 2, P, 4], BF16, name="w_group%d" % u, tag="w_group%d" % u, align_bytes=64) for u in range(2)]
         w_code = [keep.tile([P, 2 * P], U32, name="w_code%d" % u, align_bytes=64) for u in range(2)]
         w_scale = [keep.tile([P, 2 * P], U8, name="w_scale%d" % u, align_bytes=64) for u in range(2)]
-        w_cols = w_raw[:].rearrange("p j (m t) -> p m t j", t=4)
+        w_cols = w_raw[:].rearrange("p j (m t) -> p m j t", t=4)
 
         def group_w(u):
-            nc.scalar.copy(out=w_group[u][:].rearrange("p e m j -> p m e j"), in_=w_cols[:, :, 2 * u : 2 * u + 2, :])
+            nc.scalar.copy(out=w_group[u][:].rearrange("p e m j -> p m j e"), in_=w_cols[:, :, :, 2 * u : 2 * u + 2])
 
         def quantise_w(u):
             nc.vector.quantize_mx(
@@ -121,14 +109,14 @@ def tile_picked_treeup_relu_e_kernel(tc, xT, w1, w2_words, w2_scales, share, off
             )
 
         pick(1, 0, 256)
-        weave(0, 256)
+        weave(0, 0, 256, True)
         pick(1, 256, 256)
-        weave(256, 256)
+        weave(0, 256, 256, True)
         pick(1, 512, 512)
         group_w(0)
         group_w(1)
         quantise_x(0)
-        weave(512, 512)
+        weave(1, 0, 512, False)
         quantise_w(0)
         quantise_x(1)
         quantise_x(2)
@@ -136,13 +124,14 @@ def tile_picked_treeup_relu_e_kernel(tc, xT, w1, w2_words, w2_scales, share, off
         quantise_w(1)
 
         h = [keep.tile([P, S], F32, name="h%d" % t) for t in range(4)]
-        h_tail = keep.tile([P, 4, S - V0], F32, name="h_tail")
+        h_rows = keep.tile([P, 4, S], F32, name="h_rows")
 
         def layer1(t):
             w_cols_t = slice(P * (t % 2), P * (t % 2 + 1))
             groups = [[0], [1], [2], [3]] if t == 0 else [[0], [1, 2, 3]]
+            banks = []
             for group in groups:
-                bank = psum_h.tile([P, 512], F32, name="bank", tag="mx")
+                bank = psum.tile([P, 512], F32, name="bank", tag="mx")
                 first = X_CHUNKS[group[0]][0]
                 for c in group:
                     s0, n = X_CHUNKS[c]
@@ -160,93 +149,35 @@ def tile_picked_treeup_relu_e_kernel(tc, xT, w1, w2_words, w2_scales, share, off
                     nc.vector.tensor_scalar_max(h[t][:, first : first + width], bank[:, 0:width], 0.0)
                 else:
                     nc.scalar.activation(out=h[t][:, first : first + width], in_=bank[:, 0:width], func=ACT.Relu)
-            nc.sync.dma_start(out=h_tail[:, t, :], in_=h[t][:, V0:S])
+                banks.append((bank, first, width))
+            if t < 3:
+                nc.sync.dma_start(out=h_rows[:, t, :], in_=h[t][:])
+            else:
+                for bank, first, width in banks:
+                    nc.scalar.activation(out=h_rows[:, t, first : first + width], in_=bank[:, 0:width], func=ACT.Relu)
 
-        taken = [keep.tile([P, V0], F32, name="taken%d" % t) for t in range(4)]
-        turned = [[keep.tile([P, n // P, P, 2], BF16, name="turned%d_%d" % (c, u), tag="turned%d_%d" % (c, u), align_bytes=64) for u in range(2)] for c, (s0, n) in enumerate(PE_CHUNKS)]
-        z = {}
-        taken_v = {}
-
-        def new_z(c):
-            tag = "turned1_1" if c == 2 else "z%d" % c
-            z.setdefault(c, keep.tile([P, Z_CHUNKS[c][1], 4], BF16, name="z%d" % c, tag=tag, align_bytes=64))
-
-        def new_taken_v(c, u):
-            tag = {(2, 1): "share256", (3, 0): "share512", (3, 1): "taken_v2_0", (4, 0): "z1", (4, 1): "share512"}.get((c, u), "taken_v%d_%d" % (c, u))
-            taken_v.setdefault((c, u), keep.tile([P, 2, Z_CHUNKS[c][1]], F32, name="taken_v%d_%d" % (c, u), tag=tag, align_bytes=64))
-
+        taken = [keep.tile([P, 4, n], F32, name="taken%d" % c) for c, (s0, n) in enumerate(Z_CHUNKS)]
+        z = [keep.tile([P, n, 4], BF16, name="z%d" % c, align_bytes=64) for c, (s0, n) in enumerate(Z_CHUNKS)]
         z_code = [keep.tile([P, n], U32, name="z_code%d" % c, align_bytes=64) for c, (s0, n) in enumerate(Z_CHUNKS)]
         z_scale = [keep.tile([P, n], U8, name="z_scale%d" % c, align_bytes=64) for c, (s0, n) in enumerate(Z_CHUNKS)]
 
-        def follow(t, s0, n):
-            base = max(b for b in share_sb if b <= s0)
-            dst = taken[t][:, s0 : s0 + n] if s0 < V0 else taken_v[(Z_CHUNKS.index((s0, n)), t // 2)][:, t % 2, :]
+        def follow(t, c):
+            s0, n = Z_CHUNKS[c]
             nc.vector.tensor_tensor(
-                out=dst,
+                out=taken[c][:, t, :],
                 in0=h[t][:].indirect(par_sb[:, s0 // 16 : (s0 + n) // 16]),
-                in1=share_sb[base][:, s0 - base : s0 - base + n],
+                in1=share_sb[:, s0 : s0 + n],
                 op=ALU.mult,
             )
 
-        sums = {}
-
-        def turn(name, t, c):
-            source = h if name == "h" else taken
-            s0, n = PE_CHUNKS[c]
-            u, e = divmod(t, 2)
-            first = name == "h" and e == 0
-            last = name == "taken" and e == 1
-            if first:
-                pool, tag = (psum_f, "turn") if u == 0 else (psum_h, "mx")
-                sums.setdefault((u, c), pool.tile([P, n // P, 2, P], F32, name="fbank", tag=tag))
-            bank = sums[(u, c)]
-            for b in range(n // P):
-                nc.tensor.matmul(
-                    bank[:, b, e, :],
-                    lhsT=source[t][:, s0 + P * b : s0 + P * (b + 1)],
-                    rhs=ident[:],
-                    is_transpose=True,
-                    start=first and b == 0,
-                    stop=last and b == n // P - 1,
-                )
-            if last:
-                nc.scalar.copy(out=turned[c][u][:], in_=bank[:].rearrange("s b e p -> s b p e"))
-
-        def turn_back(c):
-            s0, n = PE_CHUNKS[c]
-            bank = psum_f.tile([P, n // P, 2, P], F32, name="bbank", tag="turn")
-            for b in range(n // P):
-                for u in range(2):
-                    words = turned[c][u][:, b, :, :].rearrange("s p e -> s (p e)").bitcast(F32)
-                    nc.tensor.transpose(bank[:, b, u, :], words, ident[:])
-            new_z(c)
-            z_words = z[c][:].rearrange("p n t -> p (n t)").bitcast(F32).rearrange("p (b s u) -> p b s u", u=2, s=P)
-            nc.scalar.copy(out=z_words, in_=bank[:].rearrange("p b u s -> p b s u"))
-
-        z_pairs = {}
-
-        def add(c, u):
+        def add(c):
             s0, n = Z_CHUNKS[c]
-            if u == 0:
-                tag = {2: "share0", 3: "z0", 4: "z_pairs"}[c]
-                z_pairs.setdefault(c, keep.tile([P, 2, n, 2], BF16, name="z_pairs%d" % c, tag=tag, align_bytes=64))
             nc.vector.tensor_tensor(
-                out=z_pairs[c][:, u, :, :],
-                in0=taken_v[(c, u)][:].rearrange("p e n -> p n e"),
-                in1=h_tail[:, 2 * u : 2 * u + 2, s0 - V0 : s0 - V0 + n].rearrange("p e n -> p n e"),
+                out=z[c][:].rearrange("p (c i) t -> p c t i", i=LINE),
+                in0=taken[c][:].rearrange("p t (c i) -> p c t i", i=LINE),
+                in1=h_rows[:, :, s0 : s0 + n].rearrange("p t (c i) -> p c t i", i=LINE),
                 op=ALU.add,
             )
-
-        def weave_z(c):
-            new_z(c)
-            last = c == len(Z_CHUNKS) - 1
-            word = I32 if last else U32
-            dst = z[c][:].rearrange("p n t -> p (n t)").bitcast(word).rearrange("p (n u) -> p n u", u=2)
-            src = z_pairs[c][:].rearrange("p u n e -> p (u n e)").bitcast(word).rearrange("p (u n) -> p n u", u=2)
-            if last:
-                nc.vector.tensor_copy(out=dst, in_=src)
-            else:
-                nc.scalar.copy(out=dst, in_=src)
 
         def layer2(c):
             s0, n = Z_CHUNKS[c]
@@ -255,7 +186,7 @@ def tile_picked_treeup_relu_e_kernel(tc, xT, w1, w2_words, w2_scales, share, off
             )
             groups = [[0], [1]] if c == len(Z_CHUNKS) - 1 else [[0, 1]]
             for group in groups:
-                bank = psum_h.tile([P, len(group), n], F32, name="obank", tag="mx")
+                bank = psum.tile([P, len(group), n], F32, name="obank", tag="mx")
                 for m in group:
                     nc.tensor.matmul_mx(
                         out=bank[:, m - group[0], :],
@@ -277,42 +208,17 @@ def tile_picked_treeup_relu_e_kernel(tc, xT, w1, w2_words, w2_scales, share, off
                 else:
                     nc.sync.dma_start(out=dst, in_=res[:])
 
+        chunks = range(len(Z_CHUNKS))
         for t in range(4):
             layer1(t)
-        pe = range(len(PE_CHUNKS))
-        new_taken_v(2, 0)
-        for t in range(4):
-            for c in pe:
-                follow(t, 256 * c, 256)
-            if t < 2:
-                follow(t, 512, 256)
-        for name, t in (("h", 0), ("h", 1), ("taken", 0), ("h", 2), ("taken", 1), ("h", 3), ("taken", 2), ("taken", 3)):
-            for c in pe:
-                turn(name, t, c)
-        for c in pe:
-            turn_back(c)
-        new_taken_v(2, 1)
-        follow(2, 512, 256)
-        follow(3, 512, 256)
-        add(2, 0)
-        add(2, 1)
-        weave_z(2)
-        for t in range(4):
-            if t % 2 == 0:
-                new_taken_v(3, t // 2)
-            follow(t, 768, 128)
-        layer2(0)
-        add(3, 0)
-        add(3, 1)
-        weave_z(3)
-        layer2(1)
-        for t in range(4):
-            if t % 2 == 0:
-                new_taken_v(4, t // 2)
-            follow(t, 896, 128)
-        layer2(2)
-        add(4, 0)
-        add(4, 1)
-        layer2(3)
-        weave_z(4)
-        layer2(4)
+        for t in range(3):
+            for c in chunks:
+                follow(t, c)
+        follow(3, 0)
+        for c in chunks:
+            if c + 1 in chunks:
+                follow(3, c + 1)
+            if c > 0:
+                layer2(c - 1)
+            add(c)
+        layer2(len(Z_CHUNKS) - 1)

@@ -1,6 +1,7 @@
 from contextlib import ExitStack
 
 import concourse.mybir as mybir
+from concourse.masks import make_identity
 
 K, T, S, H, N = 512, 2048, 1024, 512, 256
 P = 128
@@ -17,9 +18,13 @@ FP4X4 = mybir.dt.float4_e2m1fn_x4
 ALU = mybir.AluOpType
 ACT = mybir.ActivationFunctionType
 
-X_LOADS = [(0, 0, 1024, 768), (0, 1024, 1024, 384), (1, 0, 1024, 640), (1, 1024, 512, 256), (1, 1536, 512, 192)]
-X_CHUNKS = [(0, 512), (512, 256), (768, 128), (896, 128)]
-Z_CHUNKS = [(0, 256), (256, 256), (512, 256), (768, 128), (896, 128)]
+X_LOADS = [(0, 0, 1024, 768), (0, 1024, 1024, 384), (1, 0, 1024, 640), (1, 1024, 768, 288), (1, 1792, 256, 96)]
+X_CHUNKS = [(0, 512), (512, 256), (768, 256)]
+PE_CHUNKS = [(0, 256), (256, 256)]
+V_CHUNKS = [(512, 256), (768, 128), (896, 128)]
+V_GATHERS = [(512, 384), (896, 128)]
+Z_CHUNKS = PE_CHUNKS + V_CHUNKS
+V0 = V_CHUNKS[0][0]
 LINE = 4
 
 
@@ -33,6 +38,8 @@ def tile_picked_treeup_relu_e_kernel(tc, xT, w1, w2_words, w2_scales, share, off
         par_sb = keep.tile([P, S // 16], U16, name="par_sb")
         w2_scale = keep.tile([P, N], U8, name="w2_scale", align_bytes=64)
         nc.gpsimd.memset(w2_scale[:], 0)
+        ident = keep.tile([P, P], F32, name="ident")
+        make_identity(nc, ident[:])
 
         x_rows = xT.rearrange("(p j) t -> p j t", j=4)
         raws = []
@@ -54,7 +61,7 @@ def tile_picked_treeup_relu_e_kernel(tc, xT, w1, w2_words, w2_scales, share, off
 
         pairs = [keep.tile([P, T, 2], BF16, name="pairs%d" % u, align_bytes=64) for u in range(2)]
         got = keep.tile([P, 2, S], U32, name="got")
-        picked = [keep.tile([P, 512, 2], U32, name="picked%d" % half, align_bytes=64) for half in range(2)]
+        picked = {}
         x_code = {}
         x_scale = [keep.tile([P, n], U8, name="x_scale%d" % c, align_bytes=64) for c, (s0, n) in enumerate(X_CHUNKS)]
 
@@ -70,8 +77,11 @@ def tile_picked_treeup_relu_e_kernel(tc, xT, w1, w2_words, w2_scales, share, off
             nc.vector.tensor_copy(out=got[:, u, s0 : s0 + n], in_=window.indirect(offs_sb[:, s0 // 16 : (s0 + n) // 16]))
 
         def weave(c, a, n, on_scalar):
-            s0 = 512 * c + a
+            s0 = X_CHUNKS[c][0] + a
             word = U32 if on_scalar else I32
+            if a == 0:
+                tag = "picked0" if c == 2 else "picked%d" % c
+                picked.setdefault(c, keep.tile([P, X_CHUNKS[c][1], 2], U32, name="picked%d" % c, tag=tag, align_bytes=64))
             dst = picked[c][:].bitcast(word)[:, a : a + n, :].rearrange("p (c i) u -> p c u i", i=LINE)
             src = got[:].bitcast(word)[:, :, s0 : s0 + n].rearrange("p u (c i) -> p c u i", i=LINE)
             if on_scalar:
@@ -86,7 +96,7 @@ def tile_picked_treeup_relu_e_kernel(tc, xT, w1, w2_words, w2_scales, share, off
             nc.vector.quantize_mx(
                 out=x_code[c][:].bitcast(FP8X4),
                 scales=x_scale[c][:],
-                in_=picked[s0 // 512][:, s0 % 512 : s0 % 512 + n, :].rearrange("p n u -> p (n u)").bitcast(BF16),
+                in_=picked[c][:].rearrange("p n u -> p (n u)").bitcast(BF16),
             )
 
         for n, (u, c0, width, split) in enumerate(X_LOADS):
@@ -95,13 +105,15 @@ def tile_picked_treeup_relu_e_kernel(tc, xT, w1, w2_words, w2_scales, share, off
             if n == 1:
                 pick(0, 0, S)
 
-        w_group = [keep.tile([P, 2, P, 4], BF16, name="w_group%d" % u, tag="w_group%d" % u, align_bytes=64) for u in range(2)]
+        w_group = {}
         w_code = [keep.tile([P, 2 * P], U32, name="w_code%d" % u, align_bytes=64) for u in range(2)]
         w_scale = [keep.tile([P, 2 * P], U8, name="w_scale%d" % u, align_bytes=64) for u in range(2)]
         w_cols = w_raw[:].rearrange("p j (m t) -> p m j t", t=4)
 
-        def group_w(u):
-            nc.scalar.copy(out=w_group[u][:].rearrange("p e m j -> p m j e"), in_=w_cols[:, :, :, 2 * u : 2 * u + 2])
+        def group_w(u, engine_copy):
+            tag = "w_group0" if u == 0 else "picked1"
+            w_group.setdefault(u, keep.tile([P, 2, P, 4], BF16, name="w_group%d" % u, tag=tag, align_bytes=64))
+            engine_copy(out=w_group[u][:].rearrange("p e m j -> p m j e"), in_=w_cols[:, :, :, 2 * u : 2 * u + 2])
 
         def quantise_w(u):
             nc.vector.quantize_mx(
@@ -112,72 +124,114 @@ def tile_picked_treeup_relu_e_kernel(tc, xT, w1, w2_words, w2_scales, share, off
         weave(0, 0, 256, True)
         pick(1, 256, 256)
         weave(0, 256, 256, True)
-        pick(1, 512, 512)
-        group_w(0)
-        group_w(1)
+        pick(1, 512, 256)
+        pick(1, 768, 256)
+        group_w(0, nc.scalar.copy)
+        weave(1, 0, 256, False)
         quantise_x(0)
-        weave(1, 0, 512, False)
+        weave(2, 0, 256, True)
         quantise_w(0)
         quantise_x(1)
         quantise_x(2)
-        quantise_x(3)
+        group_w(1, nc.vector.tensor_copy)
         quantise_w(1)
 
         h = [keep.tile([P, S], F32, name="h%d" % t) for t in range(4)]
-        h_rows = keep.tile([P, 4, S], F32, name="h_rows")
+        h_rows = keep.tile([P, 4, S - V0], F32, name="h_rows")
 
         def layer1(t):
             w_cols_t = slice(P * (t % 2), P * (t % 2 + 1))
-            groups = [[0], [1], [2], [3]] if t == 0 else [[0], [1, 2, 3]]
-            banks = []
-            for group in groups:
-                bank = psum.tile([P, 512], F32, name="bank", tag="mx")
-                first = X_CHUNKS[group[0]][0]
-                for c in group:
-                    s0, n = X_CHUNKS[c]
+            width = 256 if t == 0 else 512
+            for first in range(0, S, width):
+                bank = psum.tile([P, width], F32, name="bank", tag="mx")
+                for c, (c0, cn) in enumerate(X_CHUNKS):
+                    s0 = max(c0, first)
+                    n = min(c0 + cn, first + width) - s0
+                    if n <= 0:
+                        continue
                     nc.tensor.matmul_mx(
                         out=bank[:, s0 - first : s0 - first + n],
                         lhsT=w_code[t // 2][:, w_cols_t].bitcast(FP8X4),
                         lhsT_scale=w_scale[t // 2][:, w_cols_t],
-                        rhs=x_code[c][:].bitcast(FP8X4),
-                        rhs_scale=x_scale[c][:],
+                        rhs=x_code[c][:, s0 - c0 : s0 - c0 + n].bitcast(FP8X4),
+                        rhs_scale=x_scale[c][:, s0 - c0 : s0 - c0 + n],
                         start=True,
                         stop=True,
                     )
-                width = s0 + n - first
-                if group[0] >= 2:
-                    nc.vector.tensor_scalar_max(h[t][:, first : first + width], bank[:, 0:width], 0.0)
-                else:
-                    nc.scalar.activation(out=h[t][:, first : first + width], in_=bank[:, 0:width], func=ACT.Relu)
-                banks.append((bank, first, width))
-            if t < 3:
-                nc.sync.dma_start(out=h_rows[:, t, :], in_=h[t][:])
-            else:
-                for bank, first, width in banks:
-                    nc.scalar.activation(out=h_rows[:, t, first : first + width], in_=bank[:, 0:width], func=ACT.Relu)
+                nc.scalar.activation(out=h[t][:, first : first + width], in_=bank[:, 0:width], func=ACT.Relu)
+            nc.sync.dma_start(out=h_rows[:, t, :], in_=h[t][:, V0:S])
 
-        taken = [keep.tile([P, 4, n], F32, name="taken%d" % c) for c, (s0, n) in enumerate(Z_CHUNKS)]
-        z = [keep.tile([P, n, 4], BF16, name="z%d" % c, align_bytes=64) for c, (s0, n) in enumerate(Z_CHUNKS)]
+        taken = {}
+        z = {}
         z_code = [keep.tile([P, n], U32, name="z_code%d" % c, align_bytes=64) for c, (s0, n) in enumerate(Z_CHUNKS)]
         z_scale = [keep.tile([P, n], U8, name="z_scale%d" % c, align_bytes=64) for c, (s0, n) in enumerate(Z_CHUNKS)]
+        first_v = len(PE_CHUNKS)
 
-        def follow(t, c):
-            s0, n = Z_CHUNKS[c]
+        def new_z(c):
+            z.setdefault(c, keep.tile([P, Z_CHUNKS[c][1], 4], BF16, name="z%d" % c, tag="z%d" % c, align_bytes=64))
+
+        taken_pe = keep.tile([P, 4, V0], F32, name="taken_pe")
+
+        def follow(t, s0, n, dst):
             nc.vector.tensor_tensor(
-                out=taken[c][:, t, :],
-                in0=h[t][:].indirect(par_sb[:, s0 // 16 : (s0 + n) // 16]),
-                in1=share_sb[:, s0 : s0 + n],
-                op=ALU.mult,
+                out=dst, in0=h[t][:].indirect(par_sb[:, s0 // 16 : (s0 + n) // 16]), in1=share_sb[:, s0 : s0 + n], op=ALU.mult
             )
+
+        def follow_pe(t, s0, n):
+            follow(t, s0, n, taken_pe[:, t, s0 : s0 + n])
+
+        def follow_v(g, t):
+            s0, n = V_GATHERS[g]
+            if t == 0:
+                tag = "taken0" if g == 0 else "z0"
+                taken.setdefault(g, keep.tile([P, 4, n], F32, name="taken%d" % g, tag=tag, align_bytes=64))
+            follow(t, s0, n, taken[g][:, t, :])
 
         def add(c):
             s0, n = Z_CHUNKS[c]
+            g = max(g for g, (g0, width) in enumerate(V_GATHERS) if g0 <= s0)
+            a = s0 - V_GATHERS[g][0]
+            new_z(c)
             nc.vector.tensor_tensor(
                 out=z[c][:].rearrange("p (c i) t -> p c t i", i=LINE),
-                in0=taken[c][:].rearrange("p t (c i) -> p c t i", i=LINE),
-                in1=h_rows[:, :, s0 : s0 + n].rearrange("p t (c i) -> p c t i", i=LINE),
+                in0=taken[g][:, :, a : a + n].rearrange("p t (c i) -> p c t i", i=LINE),
+                in1=h_rows[:, :, s0 - V0 : s0 - V0 + n].rearrange("p t (c i) -> p c t i", i=LINE),
                 op=ALU.add,
             )
+
+        turned = [[keep.tile([P, n // P, P, 2], BF16, name="turned%d_%d" % (c, u), align_bytes=64) for u in range(2)] for c, (s0, n) in enumerate(PE_CHUNKS)]
+        sums = {}
+
+        def turn(own, t, c):
+            s0, n = PE_CHUNKS[c]
+            u, e = divmod(t, 2)
+            first = own and e == 0
+            last = not own and e == 1
+            if first:
+                sums.setdefault((u, c), psum.tile([P, n // P, 2, P], F32, name="sum_bank", tag="mx"))
+            bank = sums[(u, c)]
+            for b in range(n // P):
+                nc.tensor.matmul(
+                    bank[:, b, e, :],
+                    lhsT=h[t][:, s0 + P * b : s0 + P * (b + 1)] if own else taken_pe[:, t, s0 + P * b : s0 + P * (b + 1)],
+                    rhs=ident[:],
+                    is_transpose=True,
+                    start=first and b == 0,
+                    stop=last and b == n // P - 1,
+                )
+            if last:
+                nc.scalar.copy(out=turned[c][u][:], in_=bank[:].rearrange("s b e p -> s b p e"))
+
+        def turn_back(c):
+            s0, n = PE_CHUNKS[c]
+            bank = psum.tile([P, n // P, 2, P], F32, name="back_bank", tag="mx")
+            for u in range(2):
+                for b in range(n // P):
+                    words = turned[c][u][:, b, :, :].rearrange("s p e -> s (p e)").bitcast(F32)
+                    nc.tensor.transpose(bank[:, b, u, :], words, ident[:])
+            new_z(c)
+            z_words = z[c][:].rearrange("p n t -> p (n t)").bitcast(F32).rearrange("p (b s u) -> p b s u", u=2, s=P)
+            nc.scalar.copy(out=z_words, in_=bank[:].rearrange("p b u s -> p b s u"))
 
         def layer2(c):
             s0, n = Z_CHUNKS[c]
@@ -208,17 +262,33 @@ def tile_picked_treeup_relu_e_kernel(tc, xT, w1, w2_words, w2_scales, share, off
                 else:
                     nc.sync.dma_start(out=dst, in_=res[:])
 
-        chunks = range(len(Z_CHUNKS))
+        pe = range(first_v)
         for t in range(4):
             layer1(t)
         for t in range(3):
-            for c in chunks:
-                follow(t, c)
-        follow(3, 0)
-        for c in chunks:
-            if c + 1 in chunks:
-                follow(3, c + 1)
+            follow_pe(t, 0, V0)
+            follow_v(0, t)
+        for s0, n in PE_CHUNKS:
+            follow_pe(3, s0, n)
+        for own, t in ((True, 0), (True, 1), (False, 0), (False, 1)):
+            for c in pe:
+                turn(own, t, c)
+        for c in pe:
+            for own, t in ((True, 2), (True, 3), (False, 2)):
+                turn(own, t, c)
+        for c in pe:
+            turn(False, 3, c)
             if c > 0:
-                layer2(c - 1)
-            add(c)
-        layer2(len(Z_CHUNKS) - 1)
+                turn_back(c - 1)
+        turn_back(first_v - 1)
+        follow_v(0, 3)
+        add(2)
+        add(3)
+        layer2(2)
+        layer2(3)
+        layer2(0)
+        layer2(1)
+        for t in range(4):
+            follow_v(1, t)
+        add(4)
+        layer2(4)

@@ -20,9 +20,9 @@ ACT = mybir.ActivationFunctionType
 
 X_LOADS = [(0, 0, 1024, 768), (0, 1024, 1024, 384), (1, 0, 1024, 640), (1, 1024, 768, 288), (1, 1792, 256, 96)]
 X_CHUNKS = [(0, 512), (512, 256), (768, 256)]
-PE_CHUNKS = [(0, 256), (256, 256)]
-V_CHUNKS = [(512, 256), (768, 128), (896, 128)]
-V_GATHERS = [(512, 384), (896, 128)]
+PE_CHUNKS = [(0, 256), (256, 256), (512, 128)]
+V_CHUNKS = [(640, 256), (896, 128)]
+V_GATHERS = V_CHUNKS
 Z_CHUNKS = PE_CHUNKS + V_CHUNKS
 V0 = V_CHUNKS[0][0]
 LINE = 4
@@ -139,10 +139,9 @@ def tile_picked_treeup_relu_e_kernel(tc, xT, w1, w2_words, w2_scales, share, off
         h = [keep.tile([P, S], F32, name="h%d" % t) for t in range(4)]
         h_rows = keep.tile([P, 4, S - V0], F32, name="h_rows")
 
-        def layer1(t):
+        def layer1(t, firsts, width):
             w_cols_t = slice(P * (t % 2), P * (t % 2 + 1))
-            width = 256 if t == 0 else 512
-            for first in range(0, S, width):
+            for first in firsts:
                 bank = psum.tile([P, width], F32, name="bank", tag="mx")
                 for c, (c0, cn) in enumerate(X_CHUNKS):
                     s0 = max(c0, first)
@@ -159,11 +158,12 @@ def tile_picked_treeup_relu_e_kernel(tc, xT, w1, w2_words, w2_scales, share, off
                         stop=True,
                     )
                 nc.scalar.activation(out=h[t][:, first : first + width], in_=bank[:, 0:width], func=ACT.Relu)
-            nc.sync.dma_start(out=h_rows[:, t, :], in_=h[t][:, V0:S])
+            if first + width == S:
+                nc.sync.dma_start(out=h_rows[:, t, :], in_=h[t][:, V0:S])
 
         taken = {}
         z = {}
-        z_code = [keep.tile([P, n], U32, name="z_code%d" % c, align_bytes=64) for c, (s0, n) in enumerate(Z_CHUNKS)]
+        z_code = {}
         z_scale = [keep.tile([P, n], U8, name="z_scale%d" % c, align_bytes=64) for c, (s0, n) in enumerate(Z_CHUNKS)]
         first_v = len(PE_CHUNKS)
 
@@ -183,7 +183,7 @@ def tile_picked_treeup_relu_e_kernel(tc, xT, w1, w2_words, w2_scales, share, off
         def follow_v(g, t):
             s0, n = V_GATHERS[g]
             if t == 0:
-                tag = "taken0" if g == 0 else "z0"
+                tag = "taken0" if g == 0 else "turned1_1"
                 taken.setdefault(g, keep.tile([P, 4, n], F32, name="taken%d" % g, tag=tag, align_bytes=64))
             follow(t, s0, n, taken[g][:, t, :])
 
@@ -199,7 +199,7 @@ def tile_picked_treeup_relu_e_kernel(tc, xT, w1, w2_words, w2_scales, share, off
                 op=ALU.add,
             )
 
-        turned = [[keep.tile([P, n // P, P, 2], BF16, name="turned%d_%d" % (c, u), align_bytes=64) for u in range(2)] for c, (s0, n) in enumerate(PE_CHUNKS)]
+        turned = [[keep.tile([P, n // P, P, 2], BF16, name="turned%d_%d" % (c, u), tag="turned%d_%d" % (c, u), align_bytes=64) for u in range(2)] for c, (s0, n) in enumerate(PE_CHUNKS)]
         sums = {}
 
         def turn(own, t, c):
@@ -235,6 +235,8 @@ def tile_picked_treeup_relu_e_kernel(tc, xT, w1, w2_words, w2_scales, share, off
 
         def layer2(c):
             s0, n = Z_CHUNKS[c]
+            tag = "turned2_1" if c == first_v else "z_code%d" % c
+            z_code.setdefault(c, keep.tile([P, n], U32, name="z_code%d" % c, tag=tag, align_bytes=64))
             nc.vector.quantize_mx(
                 out=z_code[c][:].bitcast(FP8X4), scales=z_scale[c][:], in_=z[c][:].rearrange("p n t -> p (n t)")
             )
@@ -263,32 +265,36 @@ def tile_picked_treeup_relu_e_kernel(tc, xT, w1, w2_words, w2_scales, share, off
                     nc.sync.dma_start(out=dst, in_=res[:])
 
         pe = range(first_v)
-        for t in range(4):
-            layer1(t)
-        for t in range(3):
+        layer1(0, range(0, S, 256), 256)
+        layer1(1, range(0, S, 512), 512)
+        for first in range(0, S, 512):
+            for t in (2, 3):
+                layer1(t, [first], 512)
+        for t in range(2):
             follow_pe(t, 0, V0)
             follow_v(0, t)
-        for s0, n in PE_CHUNKS:
+        for s0, n in PE_CHUNKS[:-1]:
+            follow_pe(2, s0, n)
             follow_pe(3, s0, n)
+        follow_pe(2, *PE_CHUNKS[-1])
+        follow_v(0, 2)
+        follow_v(0, 3)
+        follow_pe(3, *PE_CHUNKS[-1])
         for own, t in ((True, 0), (True, 1), (False, 0), (False, 1)):
             for c in pe:
                 turn(own, t, c)
         for c in pe:
-            for own, t in ((True, 2), (True, 3), (False, 2)):
+            for own, t in ((True, 2), (True, 3), (False, 2), (False, 3)):
                 turn(own, t, c)
-        for c in pe:
-            turn(False, 3, c)
             if c > 0:
                 turn_back(c - 1)
         turn_back(first_v - 1)
-        follow_v(0, 3)
-        add(2)
         add(3)
-        layer2(2)
-        layer2(3)
         layer2(0)
+        layer2(3)
         layer2(1)
         for t in range(4):
             follow_v(1, t)
+        layer2(2)
         add(4)
         layer2(4)

@@ -220,7 +220,10 @@ def tile_picked_treeup_relu_e_kernel(tc, xT, w1, w2_words, w2_scales, share, off
                     stop=last and b == n // P - 1,
                 )
             if last:
-                nc.scalar.copy(out=turned[c][u][:], in_=bank[:].rearrange("s b e p -> s b p e"))
+                nc.scalar.copy(
+                    out=turned[c][u][:].rearrange("s b (q i) e -> s b q e i", i=LINE),
+                    in_=bank[:].rearrange("s b e (q i) -> s b q e i", i=LINE),
+                )
 
         def turn_back(c):
             s0, n = PE_CHUNKS[c]
@@ -230,16 +233,19 @@ def tile_picked_treeup_relu_e_kernel(tc, xT, w1, w2_words, w2_scales, share, off
                     words = turned[c][u][:, b, :, :].rearrange("s p e -> s (p e)").bitcast(F32)
                     nc.tensor.transpose(bank[:, b, u, :], words, ident[:])
             new_z(c)
-            z_words = z[c][:].rearrange("p n t -> p (n t)").bitcast(F32).rearrange("p (b s u) -> p b s u", u=2, s=P)
-            nc.scalar.copy(out=z_words, in_=bank[:].rearrange("p b u s -> p b s u"))
+            z_words = z[c][:].rearrange("p n t -> p (n t)").bitcast(F32).rearrange("p (b q i u) -> p b q u i", u=2, i=LINE, q=P // LINE)
+            nc.scalar.copy(out=z_words, in_=bank[:].rearrange("p b u (q i) -> p b q u i", i=LINE))
 
-        def layer2(c):
+        def quantise_z(c):
             s0, n = Z_CHUNKS[c]
             tag = "turned2_1" if c == first_v else "z_code%d" % c
             z_code.setdefault(c, keep.tile([P, n], U32, name="z_code%d" % c, tag=tag, align_bytes=64))
             nc.vector.quantize_mx(
                 out=z_code[c][:].bitcast(FP8X4), scales=z_scale[c][:], in_=z[c][:].rearrange("p n t -> p (n t)")
             )
+
+        def layer2(c):
+            s0, n = Z_CHUNKS[c]
             groups = [[0], [1]] if c == len(Z_CHUNKS) - 1 else [[0, 1]]
             for group in groups:
                 bank = psum.tile([P, len(group), n], F32, name="obank", tag="mx")
@@ -253,9 +259,10 @@ def tile_picked_treeup_relu_e_kernel(tc, xT, w1, w2_words, w2_scales, share, off
                         start=True,
                         stop=True,
                     )
-                res = keep.tile([P, len(group), n], F32, name="res%d_%d" % (c, group[0]))
+                tag = "z4" if c == first_v - 1 else "res%d_%d" % (c, group[0])
+                res = keep.tile([P, len(group), n], F32, name="res%d_%d" % (c, group[0]), tag=tag, align_bytes=64)
                 dst = out.rearrange("(m p) s -> p m s", p=P)[:, group[0] : group[-1] + 1, s0 : s0 + n]
-                if group == [1]:
+                if group == [1] or c == first_v - 1:
                     nc.vector.tensor_copy(out=res[:], in_=bank[:])
                 else:
                     nc.scalar.copy(out=res[:], in_=bank[:])
@@ -290,11 +297,13 @@ def tile_picked_treeup_relu_e_kernel(tc, xT, w1, w2_words, w2_scales, share, off
                 turn_back(c - 1)
         turn_back(first_v - 1)
         add(3)
-        layer2(0)
-        layer2(3)
-        layer2(1)
+        for c in (0, 3, 1):
+            quantise_z(c)
+            layer2(c)
         for t in range(4):
             follow_v(1, t)
-        layer2(2)
+        quantise_z(2)
         add(4)
+        quantise_z(4)
+        layer2(2)
         layer2(4)

@@ -20,11 +20,15 @@ ACT = mybir.ActivationFunctionType
 
 X_LOADS = [(0, 0, 1024, 768), (0, 1024, 1024, 384), (1, 0, 1024, 640), (1, 1024, 768, 288), (1, 1792, 256, 96)]
 X_CHUNKS = [(0, 512), (512, 256), (768, 256)]
+QUARTER = S // 4
+HALF = S // 2
 PE_CHUNKS = [(0, 256), (256, 256), (512, 128)]
 V_CHUNKS = [(640, 256), (896, 128)]
-V_GATHERS = V_CHUNKS
 Z_CHUNKS = PE_CHUNKS + V_CHUNKS
 V0 = V_CHUNKS[0][0]
+LAST_PE = len(PE_CHUNKS) - 1
+FIRST_V = len(PE_CHUNKS)
+LAST_V = len(Z_CHUNKS) - 1
 LINE = 4
 
 
@@ -43,11 +47,11 @@ def tile_picked_treeup_relu_e_kernel(tc, xT, w1, w2_words, w2_scales, share, off
 
         x_rows = xT.rearrange("(p j) t -> p j t", j=4)
         raws = []
-        for n, (u, c0, width, split) in enumerate(X_LOADS):
-            raw = keep.tile([P, 2, width], F32, name="raw%d" % n)
+        for load, (u, c0, width, split) in enumerate(X_LOADS):
+            raw = keep.tile([P, 2, width], F32, name="raw%d" % load)
             nc.sync.dma_start(out=raw[:], in_=x_rows[:, 2 * u : 2 * u + 2, c0 : c0 + width])
             raws.append(raw)
-            if n == 0:
+            if load == 0:
                 nc.sync.dma_start(offs_sb[:], offs)
         w_raw = keep.tile([P, 4, H], F32, name="w_raw")
         nc.sync.dma_start(out=w_raw[:], in_=w1.rearrange("(p j) c -> p j c", j=4))
@@ -65,44 +69,43 @@ def tile_picked_treeup_relu_e_kernel(tc, xT, w1, w2_words, w2_scales, share, off
         x_code = {}
         x_scale = [keep.tile([P, n], U8, name="x_scale%d" % c, align_bytes=64) for c, (s0, n) in enumerate(X_CHUNKS)]
 
-        def cast(engine_copy, n, a, b):
-            u, c0, width, split = X_LOADS[n]
+        def cast(engine_copy, load, a, b):
+            u, c0, width, split = X_LOADS[load]
             engine_copy(
-                out=pairs[u][:, c0 + a : c0 + b, :].rearrange("p (c i) j -> p c j i", i=LINE),
-                in_=raws[n][:, :, a:b].rearrange("p j (c i) -> p c j i", i=LINE),
+                out=pairs[u][:, c0 + a : c0 + b, :].rearrange("p (r i) j -> p r j i", i=LINE),
+                in_=raws[load][:, :, a:b].rearrange("p j (r i) -> p r j i", i=LINE),
             )
 
         def pick(u, s0, n):
             window = pairs[u][:].rearrange("p t j -> p (t j)").bitcast(U32)
             nc.vector.tensor_copy(out=got[:, u, s0 : s0 + n], in_=window.indirect(offs_sb[:, s0 // 16 : (s0 + n) // 16]))
 
-        def weave(c, a, n, on_scalar):
-            s0 = X_CHUNKS[c][0] + a
+        def weave(c, a, on_scalar):
+            s0, n = X_CHUNKS[c][0] + a, QUARTER
             word = U32 if on_scalar else I32
             if a == 0:
                 tag = "picked0" if c == 2 else "picked%d" % c
                 picked.setdefault(c, keep.tile([P, X_CHUNKS[c][1], 2], U32, name="picked%d" % c, tag=tag, align_bytes=64))
-            dst = picked[c][:].bitcast(word)[:, a : a + n, :].rearrange("p (c i) u -> p c u i", i=LINE)
-            src = got[:].bitcast(word)[:, :, s0 : s0 + n].rearrange("p u (c i) -> p c u i", i=LINE)
+            dst = picked[c][:].bitcast(word)[:, a : a + n, :].rearrange("p (r i) u -> p r u i", i=LINE)
+            src = got[:].bitcast(word)[:, :, s0 : s0 + n].rearrange("p u (r i) -> p r u i", i=LINE)
             if on_scalar:
                 nc.scalar.copy(out=dst, in_=src)
             else:
                 nc.vector.tensor_copy(out=dst, in_=src)
 
         def quantise_x(c):
-            s0, n = X_CHUNKS[c]
             tag = "w_group0" if c == 1 else "x_code%d" % c
-            x_code.setdefault(c, keep.tile([P, n], U32, name="x_code%d" % c, tag=tag, align_bytes=64))
+            x_code.setdefault(c, keep.tile([P, X_CHUNKS[c][1]], U32, name="x_code%d" % c, tag=tag, align_bytes=64))
             nc.vector.quantize_mx(
                 out=x_code[c][:].bitcast(FP8X4),
                 scales=x_scale[c][:],
                 in_=picked[c][:].rearrange("p n u -> p (n u)").bitcast(BF16),
             )
 
-        for n, (u, c0, width, split) in enumerate(X_LOADS):
-            cast(nc.scalar.copy, n, 0, split)
-            cast(nc.vector.tensor_copy, n, split, width)
-            if n == 1:
+        for load, (u, c0, width, split) in enumerate(X_LOADS):
+            cast(nc.scalar.copy, load, 0, split)
+            cast(nc.vector.tensor_copy, load, split, width)
+            if u == 0 and c0 + width == T:
                 pick(0, 0, S)
 
         w_group = {}
@@ -120,16 +123,14 @@ def tile_picked_treeup_relu_e_kernel(tc, xT, w1, w2_words, w2_scales, share, off
                 out=w_code[u][:].bitcast(FP8X4), scales=w_scale[u][:], in_=w_group[u][:].rearrange("p e m j -> p (e m j)")
             )
 
-        pick(1, 0, 256)
-        weave(0, 0, 256, True)
-        pick(1, 256, 256)
-        weave(0, 256, 256, True)
-        pick(1, 512, 256)
-        pick(1, 768, 256)
+        for s0 in range(0, S, QUARTER):
+            pick(1, s0, QUARTER)
+            if s0 < HALF:
+                weave(0, s0, True)
         group_w(0, nc.scalar.copy)
-        weave(1, 0, 256, False)
+        weave(1, 0, False)
         quantise_x(0)
-        weave(2, 0, 256, True)
+        weave(2, 0, True)
         quantise_w(0)
         quantise_x(1)
         quantise_x(2)
@@ -165,7 +166,6 @@ def tile_picked_treeup_relu_e_kernel(tc, xT, w1, w2_words, w2_scales, share, off
         z = {}
         z_code = {}
         z_scale = [keep.tile([P, n], U8, name="z_scale%d" % c, align_bytes=64) for c, (s0, n) in enumerate(Z_CHUNKS)]
-        first_v = len(PE_CHUNKS)
 
         def new_z(c):
             z.setdefault(c, keep.tile([P, Z_CHUNKS[c][1], 4], BF16, name="z%d" % c, tag="z%d" % c, align_bytes=64))
@@ -180,26 +180,28 @@ def tile_picked_treeup_relu_e_kernel(tc, xT, w1, w2_words, w2_scales, share, off
         def follow_pe(t, s0, n):
             follow(t, s0, n, taken_pe[:, t, s0 : s0 + n])
 
-        def follow_v(g, t):
-            s0, n = V_GATHERS[g]
+        def follow_v(v, t):
+            s0, n = V_CHUNKS[v]
             if t == 0:
-                tag = "taken0" if g == 0 else "turned1_1"
-                taken.setdefault(g, keep.tile([P, 4, n], F32, name="taken%d" % g, tag=tag, align_bytes=64))
-            follow(t, s0, n, taken[g][:, t, :])
+                tag = "taken0" if v == 0 else "turned1_1"
+                taken.setdefault(v, keep.tile([P, 4, n], F32, name="taken%d" % v, tag=tag, align_bytes=64))
+            follow(t, s0, n, taken[v][:, t, :])
 
         def add(c):
             s0, n = Z_CHUNKS[c]
-            g = max(g for g, (g0, width) in enumerate(V_GATHERS) if g0 <= s0)
-            a = s0 - V_GATHERS[g][0]
             new_z(c)
-            nc.vector.tensor_tensor(
-                out=z[c][:].rearrange("p (c i) t -> p c t i", i=LINE),
-                in0=taken[g][:, :, a : a + n].rearrange("p t (c i) -> p c t i", i=LINE),
-                in1=h_rows[:, :, s0 - V0 : s0 - V0 + n].rearrange("p t (c i) -> p c t i", i=LINE),
-                op=ALU.add,
-            )
+            for a in range(0, n, P):
+                nc.vector.tensor_tensor(
+                    out=z[c][:, a : a + P, :].rearrange("p (r i) t -> p r t i", i=LINE),
+                    in0=taken[c - FIRST_V][:, :, a : a + P].rearrange("p t (r i) -> p r t i", i=LINE),
+                    in1=h_rows[:, :, s0 - V0 + a : s0 - V0 + a + P].rearrange("p t (r i) -> p r t i", i=LINE),
+                    op=ALU.add,
+                )
 
-        turned = [[keep.tile([P, n // P, P, 2], BF16, name="turned%d_%d" % (c, u), tag="turned%d_%d" % (c, u), align_bytes=64) for u in range(2)] for c, (s0, n) in enumerate(PE_CHUNKS)]
+        turned = [
+            [keep.tile([P, n // P, P, 2], BF16, name="turned%d_%d" % (c, u), tag="turned%d_%d" % (c, u), align_bytes=64) for u in range(2)]
+            for c, (s0, n) in enumerate(PE_CHUNKS)
+        ]
         sums = {}
 
         def turn(own, t, c):
@@ -221,32 +223,31 @@ def tile_picked_treeup_relu_e_kernel(tc, xT, w1, w2_words, w2_scales, share, off
                 )
             if last:
                 nc.scalar.copy(
-                    out=turned[c][u][:].rearrange("s b (q i) e -> s b q e i", i=LINE),
-                    in_=bank[:].rearrange("s b e (q i) -> s b q e i", i=LINE),
+                    out=turned[c][u][:].rearrange("s b (r i) e -> s b r e i", i=LINE),
+                    in_=bank[:].rearrange("s b e (r i) -> s b r e i", i=LINE),
                 )
 
         def turn_back(c):
-            s0, n = PE_CHUNKS[c]
+            n = PE_CHUNKS[c][1]
             bank = psum.tile([P, n // P, 2, P], F32, name="back_bank", tag="mx")
             for u in range(2):
                 for b in range(n // P):
                     words = turned[c][u][:, b, :, :].rearrange("s p e -> s (p e)").bitcast(F32)
                     nc.tensor.transpose(bank[:, b, u, :], words, ident[:])
             new_z(c)
-            z_words = z[c][:].rearrange("p n t -> p (n t)").bitcast(F32).rearrange("p (b q i u) -> p b q u i", u=2, i=LINE, q=P // LINE)
-            nc.scalar.copy(out=z_words, in_=bank[:].rearrange("p b u (q i) -> p b q u i", i=LINE))
+            z_words = z[c][:].rearrange("p n t -> p (n t)").bitcast(F32).rearrange("p (b r i u) -> p b r u i", u=2, i=LINE, r=P // LINE)
+            nc.scalar.copy(out=z_words, in_=bank[:].rearrange("p b u (r i) -> p b r u i", i=LINE))
 
         def quantise_z(c):
-            s0, n = Z_CHUNKS[c]
-            tag = "turned2_1" if c == first_v else "z_code%d" % c
-            z_code.setdefault(c, keep.tile([P, n], U32, name="z_code%d" % c, tag=tag, align_bytes=64))
+            tag = "turned2_1" if c == FIRST_V else "z_code%d" % c
+            z_code.setdefault(c, keep.tile([P, Z_CHUNKS[c][1]], U32, name="z_code%d" % c, tag=tag, align_bytes=64))
             nc.vector.quantize_mx(
                 out=z_code[c][:].bitcast(FP8X4), scales=z_scale[c][:], in_=z[c][:].rearrange("p n t -> p (n t)")
             )
 
         def layer2(c):
             s0, n = Z_CHUNKS[c]
-            groups = [[0], [1]] if c == len(Z_CHUNKS) - 1 else [[0, 1]]
+            groups = [[0], [1]] if c == LAST_V else [[0, 1]]
             for group in groups:
                 bank = psum.tile([P, len(group), n], F32, name="obank", tag="mx")
                 for m in group:
@@ -259,10 +260,10 @@ def tile_picked_treeup_relu_e_kernel(tc, xT, w1, w2_words, w2_scales, share, off
                         start=True,
                         stop=True,
                     )
-                tag = "z4" if c == first_v - 1 else "res%d_%d" % (c, group[0])
+                tag = "z%d" % LAST_V if c == LAST_PE else "res%d_%d" % (c, group[0])
                 res = keep.tile([P, len(group), n], F32, name="res%d_%d" % (c, group[0]), tag=tag, align_bytes=64)
                 dst = out.rearrange("(m p) s -> p m s", p=P)[:, group[0] : group[-1] + 1, s0 : s0 + n]
-                if group == [1] or c == first_v - 1:
+                if group == [1] or c == LAST_PE:
                     nc.vector.tensor_copy(out=res[:], in_=bank[:])
                 else:
                     nc.scalar.copy(out=res[:], in_=bank[:])
@@ -271,22 +272,22 @@ def tile_picked_treeup_relu_e_kernel(tc, xT, w1, w2_words, w2_scales, share, off
                 else:
                     nc.sync.dma_start(out=dst, in_=res[:])
 
-        pe = range(first_v)
-        layer1(0, range(0, S, 256), 256)
-        layer1(1, range(0, S, 512), 512)
-        for first in range(0, S, 512):
+        pe = range(len(PE_CHUNKS))
+        layer1(0, range(0, S, QUARTER), QUARTER)
+        layer1(1, range(0, S, HALF), HALF)
+        for first, width in X_CHUNKS:
             for t in (2, 3):
-                layer1(t, [first], 512)
-        for t in range(2):
+                layer1(t, [first], width)
+
+        for t in (0, 1):
             follow_pe(t, 0, V0)
             follow_v(0, t)
-        for s0, n in PE_CHUNKS[:-1]:
+        for s0, n in PE_CHUNKS:
             follow_pe(2, s0, n)
             follow_pe(3, s0, n)
-        follow_pe(2, *PE_CHUNKS[-1])
         follow_v(0, 2)
-        follow_v(0, 3)
-        follow_pe(3, *PE_CHUNKS[-1])
+        for a in range(0, V_CHUNKS[0][1], P):
+            follow(3, V0 + a, P, taken[0][:, 3, a : a + P])
         for own, t in ((True, 0), (True, 1), (False, 0), (False, 1)):
             for c in pe:
                 turn(own, t, c)
@@ -295,15 +296,16 @@ def tile_picked_treeup_relu_e_kernel(tc, xT, w1, w2_words, w2_scales, share, off
                 turn(own, t, c)
             if c > 0:
                 turn_back(c - 1)
-        turn_back(first_v - 1)
-        add(3)
-        for c in (0, 3, 1):
+        turn_back(LAST_PE)
+
+        add(FIRST_V)
+        for c in (0, FIRST_V, 1):
             quantise_z(c)
             layer2(c)
         for t in range(4):
             follow_v(1, t)
-        quantise_z(2)
-        add(4)
-        quantise_z(4)
-        layer2(2)
-        layer2(4)
+        quantise_z(LAST_PE)
+        add(LAST_V)
+        quantise_z(LAST_V)
+        layer2(LAST_PE)
+        layer2(LAST_V)

@@ -135,7 +135,6 @@ def tile_picked_treeup_relu_e_kernel(tc, xT, w1, w2_words, w2_scales, share, off
         quantise_x(1)
         quantise_x(2)
         group_w(1, nc.vector.tensor_copy)
-        quantise_w(1)
 
         h = [keep.tile([P, S], F32, name="h%d" % t) for t in range(4)]
         h_rows = keep.tile([P, 4, S - V0], F32, name="h_rows")
@@ -158,7 +157,10 @@ def tile_picked_treeup_relu_e_kernel(tc, xT, w1, w2_words, w2_scales, share, off
                         start=True,
                         stop=True,
                     )
-                nc.scalar.activation(out=h[t][:, first : first + width], in_=bank[:, 0:width], func=ACT.Relu)
+                if (t, first) == (0, QUARTER):
+                    nc.vector.tensor_scalar(out=h[t][:, first : first + width], in0=bank[:, 0:width], scalar1=0.0, scalar2=None, op0=ALU.max)
+                else:
+                    nc.scalar.activation(out=h[t][:, first : first + width], in_=bank[:, 0:width], func=ACT.Relu)
             if first + width == S:
                 nc.sync.dma_start(out=h_rows[:, t, :], in_=h[t][:, V0:S])
 
@@ -274,6 +276,7 @@ def tile_picked_treeup_relu_e_kernel(tc, xT, w1, w2_words, w2_scales, share, off
 
         pe = range(len(PE_CHUNKS))
         layer1(0, range(0, S, QUARTER), QUARTER)
+        quantise_w(1)
         layer1(1, range(0, S, HALF), HALF)
         for first, width in X_CHUNKS:
             for t in (2, 3):

@@ -18,8 +18,9 @@ FP4X4 = mybir.dt.float4_e2m1fn_x4
 ALU = mybir.AluOpType
 ACT = mybir.ActivationFunctionType
 
-X_LOADS = [(0, 0, 1024, 768), (0, 1024, 1024, 384), (1, 0, 1024, 640), (1, 1024, 768, 288), (1, 1792, 256, 96)]
-X_CHUNKS = [(0, 512), (512, 256), (768, 256)]
+ROWS_2 = [(384, 256), (640, 256), (896, 128)]
+X_CHUNKS = [(s0, 256) for s0 in range(0, S, 256)]
+H_CHUNKS = [(0, 512), (512, 256), (768, 256)]
 QUARTER = S // 4
 HALF = S // 2
 PE_CHUNKS = [(0, 256), (256, 256), (512, 128)]
@@ -44,14 +45,16 @@ def tile_picked_treeup_relu_e_kernel(tc, xT, w1, w2_words, w2_scales, share, off
         nc.gpsimd.memset(w2_scale[:], 0)
         ident = keep.tile([P, P], F32, name="ident")
         make_identity(nc, ident[:])
+        warm_in = keep.tile([P, 1], F32, name="warm_in")
+        warm_out = keep.tile([P, 1], F32, name="warm_out")
+        nc.vector.memset(warm_in[:], 0.0)
+        nc.scalar.activation(out=warm_out[:], in_=warm_in[:], func=ACT.Relu)
 
         x_rows = xT.rearrange("(p j) t -> p j t", j=4)
-        raws = []
-        for load, (u, c0, width, split) in enumerate(X_LOADS):
-            raw = keep.tile([P, 2, width], F32, name="raw%d" % load)
-            nc.sync.dma_start(out=raw[:], in_=x_rows[:, 2 * u : 2 * u + 2, c0 : c0 + width])
-            raws.append(raw)
-            if load == 0:
+        raw = [keep.tile([P, T], F32, name="raw%d" % j) for j in range(4)]
+        for j in range(4):
+            nc.sync.dma_start(out=raw[j][:], in_=x_rows[:, j, :])
+            if j == 0:
                 nc.sync.dma_start(offs_sb[:], offs)
         w_raw = keep.tile([P, 4, H], F32, name="w_raw")
         nc.sync.dma_start(out=w_raw[:], in_=w1.rearrange("(p j) c -> p j c", j=4))
@@ -63,50 +66,37 @@ def tile_picked_treeup_relu_e_kernel(tc, xT, w1, w2_words, w2_scales, share, off
         for q in range(4):
             nc.sync.dma_start(out=w2_scale[32 * q : 32 * q + 4, :].bitcast(I32), in_=w2_scales[0, 4 * q : 4 * q + 4, :].bitcast(I32))
 
-        pairs = [keep.tile([P, T, 2], BF16, name="pairs%d" % u, align_bytes=64) for u in range(2)]
-        got = keep.tile([P, 2, S], U32, name="got")
-        picked = {}
-        x_code = {}
-        x_scale = [keep.tile([P, n], U8, name="x_scale%d" % c, align_bytes=64) for c, (s0, n) in enumerate(X_CHUNKS)]
+        got = [keep.tile([P, 2, S], BF16, name="got%d" % u, tag="got%d" % u, align_bytes=64) for u in range(2)]
+        picked = keep.tile([P, S, 4], BF16, name="picked", align_bytes=64)
+        x_code = keep.tile([P, S], U32, name="x_code", align_bytes=64)
+        x_scale = keep.tile([P, S], U8, name="x_scale", align_bytes=64)
 
-        def cast(engine_copy, load, a, b):
-            u, c0, width, split = X_LOADS[load]
-            engine_copy(
-                out=pairs[u][:, c0 + a : c0 + b, :].rearrange("p (r i) j -> p r j i", i=LINE),
-                in_=raws[load][:, :, a:b].rearrange("p j (r i) -> p r j i", i=LINE),
-            )
-
-        def pick(u, s0, n):
-            window = pairs[u][:].rearrange("p t j -> p (t j)").bitcast(U32)
-            nc.vector.tensor_copy(out=got[:, u, s0 : s0 + n], in_=window.indirect(offs_sb[:, s0 // 16 : (s0 + n) // 16]))
-
-        def weave(c, a, on_scalar):
-            s0, n = X_CHUNKS[c][0] + a, QUARTER
-            word = U32 if on_scalar else I32
-            if a == 0:
-                tag = "picked0" if c == 2 else "picked%d" % c
-                picked.setdefault(c, keep.tile([P, X_CHUNKS[c][1], 2], U32, name="picked%d" % c, tag=tag, align_bytes=64))
-            dst = picked[c][:].bitcast(word)[:, a : a + n, :].rearrange("p (r i) u -> p r u i", i=LINE)
-            src = got[:].bitcast(word)[:, :, s0 : s0 + n].rearrange("p u (r i) -> p r u i", i=LINE)
-            if on_scalar:
-                nc.scalar.copy(out=dst, in_=src)
-            else:
-                nc.vector.tensor_copy(out=dst, in_=src)
+        def offsets(list_sb, s0, n):
+            return list_sb[:, s0 // 16 : (s0 + n) // 16]
 
         def quantise_x(c):
-            tag = "w_group0" if c == 1 else "x_code%d" % c
-            x_code.setdefault(c, keep.tile([P, X_CHUNKS[c][1]], U32, name="x_code%d" % c, tag=tag, align_bytes=64))
+            s0, n = X_CHUNKS[c]
             nc.vector.quantize_mx(
-                out=x_code[c][:].bitcast(FP8X4),
-                scales=x_scale[c][:],
-                in_=picked[c][:].rearrange("p n u -> p (n u)").bitcast(BF16),
+                out=x_code[:, s0 : s0 + n].bitcast(FP8X4),
+                scales=x_scale[:, s0 : s0 + n],
+                in_=picked[:, s0 : s0 + n, :].rearrange("p n j -> p (n j)"),
             )
 
-        for load, (u, c0, width, split) in enumerate(X_LOADS):
-            cast(nc.scalar.copy, load, 0, split)
-            cast(nc.vector.tensor_copy, load, split, width)
-            if u == 0 and c0 + width == T:
-                pick(0, 0, S)
+        def pick_in_place(j, n):
+            nc.vector.tensor_copy(out=picked[:, 0:n, j], in_=raw[j][:].indirect(offsets(offs_sb, 0, n)))
+
+        def pick_row(j, s0, n):
+            nc.scalar.activation(out=got[j // 2][:, j % 2, s0 : s0 + n], in_=raw[j][:].indirect(offsets(offs_sb, s0, n)), func=ACT.Copy)
+
+        for j in (0, 1):
+            pick_in_place(j, HALF)
+            pick_row(j, HALF, HALF)
+        nc.vector.tensor_copy(out=picked[:, HALF:S, 0:2], in_=got[0][:, :, HALF:S].rearrange("p e n -> p n e"))
+        for j, pieces in ((2, ROWS_2), (3, X_CHUNKS[1:])):
+            pick_in_place(j, pieces[0][0])
+            for s0, n in pieces:
+                pick_row(j, s0, n)
+                nc.vector.tensor_copy(out=picked[:, s0 : s0 + n, j], in_=got[1][:, j % 2, s0 : s0 + n])
 
         w_group = {}
         w_code = [keep.tile([P, 2 * P], U32, name="w_code%d" % u, align_bytes=64) for u in range(2)]
@@ -114,8 +104,7 @@ def tile_picked_treeup_relu_e_kernel(tc, xT, w1, w2_words, w2_scales, share, off
         w_cols = w_raw[:].rearrange("p j (m t) -> p m j t", t=4)
 
         def group_w(u, engine_copy):
-            tag = "w_group0" if u == 0 else "picked1"
-            w_group.setdefault(u, keep.tile([P, 2, P, 4], BF16, name="w_group%d" % u, tag=tag, align_bytes=64))
+            w_group.setdefault(u, keep.tile([P, 2, P, 4], BF16, name="w_group%d" % u, tag="w_group", align_bytes=64))
             engine_copy(out=w_group[u][:].rearrange("p e m j -> p m j e"), in_=w_cols[:, :, :, 2 * u : 2 * u + 2])
 
         def quantise_w(u):
@@ -123,17 +112,10 @@ def tile_picked_treeup_relu_e_kernel(tc, xT, w1, w2_words, w2_scales, share, off
                 out=w_code[u][:].bitcast(FP8X4), scales=w_scale[u][:], in_=w_group[u][:].rearrange("p e m j -> p (e m j)")
             )
 
-        for s0 in range(0, S, QUARTER):
-            pick(1, s0, QUARTER)
-            if s0 < HALF:
-                weave(0, s0, True)
+        for c in range(len(X_CHUNKS)):
+            quantise_x(c)
         group_w(0, nc.scalar.copy)
-        weave(1, 0, False)
-        quantise_x(0)
-        weave(2, 0, True)
         quantise_w(0)
-        quantise_x(1)
-        quantise_x(2)
         group_w(1, nc.vector.tensor_copy)
 
         h = [keep.tile([P, S], F32, name="h%d" % t) for t in range(4)]
@@ -143,20 +125,15 @@ def tile_picked_treeup_relu_e_kernel(tc, xT, w1, w2_words, w2_scales, share, off
             w_cols_t = slice(P * (t % 2), P * (t % 2 + 1))
             for first in firsts:
                 bank = psum.tile([P, width], F32, name="bank", tag="mx")
-                for c, (c0, cn) in enumerate(X_CHUNKS):
-                    s0 = max(c0, first)
-                    n = min(c0 + cn, first + width) - s0
-                    if n <= 0:
-                        continue
-                    nc.tensor.matmul_mx(
-                        out=bank[:, s0 - first : s0 - first + n],
-                        lhsT=w_code[t // 2][:, w_cols_t].bitcast(FP8X4),
-                        lhsT_scale=w_scale[t // 2][:, w_cols_t],
-                        rhs=x_code[c][:, s0 - c0 : s0 - c0 + n].bitcast(FP8X4),
-                        rhs_scale=x_scale[c][:, s0 - c0 : s0 - c0 + n],
-                        start=True,
-                        stop=True,
-                    )
+                nc.tensor.matmul_mx(
+                    out=bank[:],
+                    lhsT=w_code[t // 2][:, w_cols_t].bitcast(FP8X4),
+                    lhsT_scale=w_scale[t // 2][:, w_cols_t],
+                    rhs=x_code[:, first : first + width].bitcast(FP8X4),
+                    rhs_scale=x_scale[:, first : first + width],
+                    start=True,
+                    stop=True,
+                )
                 if (t, first) == (0, QUARTER):
                     nc.vector.tensor_scalar(out=h[t][:, first : first + width], in0=bank[:, 0:width], scalar1=0.0, scalar2=None, op0=ALU.max)
                 else:
@@ -176,7 +153,7 @@ def tile_picked_treeup_relu_e_kernel(tc, xT, w1, w2_words, w2_scales, share, off
 
         def follow(t, s0, n, dst):
             nc.vector.tensor_tensor(
-                out=dst, in0=h[t][:].indirect(par_sb[:, s0 // 16 : (s0 + n) // 16]), in1=share_sb[:, s0 : s0 + n], op=ALU.mult
+                out=dst, in0=h[t][:].indirect(offsets(par_sb, s0, n)), in1=share_sb[:, s0 : s0 + n], op=ALU.mult
             )
 
         def follow_pe(t, s0, n):
@@ -278,7 +255,7 @@ def tile_picked_treeup_relu_e_kernel(tc, xT, w1, w2_words, w2_scales, share, off
         layer1(0, range(0, S, QUARTER), QUARTER)
         quantise_w(1)
         layer1(1, range(0, S, HALF), HALF)
-        for first, width in X_CHUNKS:
+        for first, width in H_CHUNKS:
             for t in (2, 3):
                 layer1(t, [first], width)
 

@@ -18,8 +18,10 @@ FP4X4 = mybir.dt.float4_e2m1fn_x4
 ALU = mybir.AluOpType
 ACT = mybir.ActivationFunctionType
 
-ROWS_2 = [(384, 256), (640, 256), (896, 128)]
-X_CHUNKS = [(s0, 256) for s0 in range(0, S, 256)]
+X_ROWS = {2: [(384, 256), (640, 128), (768, 256)], 3: [(512, 256), (768, 256)]}
+X_CHUNKS = [(0, 512), (512, 256), (768, 256)]
+W_SPLIT = 76
+W_SPLIT_1 = 96
 H_CHUNKS = [(0, 512), (512, 256), (768, 256)]
 QUARTER = S // 4
 HALF = S // 2
@@ -30,6 +32,9 @@ V0 = V_CHUNKS[0][0]
 LAST_PE = len(PE_CHUNKS) - 1
 FIRST_V = len(PE_CHUNKS)
 LAST_V = len(Z_CHUNKS) - 1
+SUM_BANKS = [(1, 2, 4), (5, 6, 7)]
+BACK_BANKS = (0, 3, 1)
+OUT_BANKS = (2, 5, 6, 4, 0)
 LINE = 4
 
 
@@ -37,7 +42,7 @@ def tile_picked_treeup_relu_e_kernel(tc, xT, w1, w2_words, w2_scales, share, off
     nc = tc.nc
     with ExitStack() as ctx:
         keep = ctx.enter_context(tc.tile_pool(name="keep", bufs=1))
-        psum = ctx.enter_context(tc.psum_pool(name="psum", bufs=8))
+        psum = ctx.enter_context(tc.psum_pool(name="psum", bufs=1))
 
         offs_sb = keep.tile([P, S // 16], U16, name="offs_sb")
         par_sb = keep.tile([P, S // 16], U16, name="par_sb")
@@ -67,8 +72,8 @@ def tile_picked_treeup_relu_e_kernel(tc, xT, w1, w2_words, w2_scales, share, off
             nc.sync.dma_start(out=w2_scale[32 * q : 32 * q + 4, :].bitcast(I32), in_=w2_scales[0, 4 * q : 4 * q + 4, :].bitcast(I32))
 
         got = [keep.tile([P, 2, S], BF16, name="got%d" % u, tag="got%d" % u, align_bytes=64) for u in range(2)]
-        picked = keep.tile([P, S, 4], BF16, name="picked", align_bytes=64)
-        x_code = keep.tile([P, S], U32, name="x_code", align_bytes=64)
+        picked = keep.tile([P, S, 4], BF16, name="picked", tag="picked", align_bytes=64)
+        x_code = {}
         x_scale = keep.tile([P, S], U8, name="x_scale", align_bytes=64)
 
         def offsets(list_sb, s0, n):
@@ -76,8 +81,11 @@ def tile_picked_treeup_relu_e_kernel(tc, xT, w1, w2_words, w2_scales, share, off
 
         def quantise_x(c):
             s0, n = X_CHUNKS[c]
+            half, a = divmod(s0, HALF)
+            if a == 0:
+                x_code.setdefault(half, keep.tile([P, HALF], U32, name="x_code%d" % half, tag=("x_code0", "w_group0")[half], align_bytes=64))
             nc.vector.quantize_mx(
-                out=x_code[:, s0 : s0 + n].bitcast(FP8X4),
+                out=x_code[half][:, a : a + n].bitcast(FP8X4),
                 scales=x_scale[:, s0 : s0 + n],
                 in_=picked[:, s0 : s0 + n, :].rearrange("p n j -> p (n j)"),
             )
@@ -92,49 +100,58 @@ def tile_picked_treeup_relu_e_kernel(tc, xT, w1, w2_words, w2_scales, share, off
             pick_in_place(j, HALF)
             pick_row(j, HALF, HALF)
         nc.vector.tensor_copy(out=picked[:, HALF:S, 0:2], in_=got[0][:, :, HALF:S].rearrange("p e n -> p n e"))
-        for j, pieces in ((2, ROWS_2), (3, X_CHUNKS[1:])):
+        for j, pieces in X_ROWS.items():
             pick_in_place(j, pieces[0][0])
             for s0, n in pieces:
                 pick_row(j, s0, n)
-                nc.vector.tensor_copy(out=picked[:, s0 : s0 + n, j], in_=got[1][:, j % 2, s0 : s0 + n])
+                if s0 + n < S:
+                    nc.vector.tensor_copy(out=picked[:, s0 : s0 + n, j], in_=got[1][:, j % 2, s0 : s0 + n])
+        s0 = S - QUARTER
+        nc.scalar.copy(out=picked[:, s0:S, 2:4], in_=got[1][:, :, s0:S].rearrange("p e n -> p n e"))
 
-        w_group = {}
-        w_code = [keep.tile([P, 2 * P], U32, name="w_code%d" % u, align_bytes=64) for u in range(2)]
+        w_group = [keep.tile([P, 2, P, 4], BF16, name="w_group%d" % u, tag="w_group%d" % u, align_bytes=64) for u in range(2)]
+        w_code = [keep.tile([P, 2 * P], U32, name="w_code%d" % u, tag=("w_code0", "picked")[u], align_bytes=64) for u in range(2)]
         w_scale = [keep.tile([P, 2 * P], U8, name="w_scale%d" % u, align_bytes=64) for u in range(2)]
         w_cols = w_raw[:].rearrange("p j (m t) -> p m j t", t=4)
 
-        def group_w(u, engine_copy):
-            w_group.setdefault(u, keep.tile([P, 2, P, 4], BF16, name="w_group%d" % u, tag="w_group", align_bytes=64))
-            engine_copy(out=w_group[u][:].rearrange("p e m j -> p m j e"), in_=w_cols[:, :, :, 2 * u : 2 * u + 2])
+        def group_w(u, engine_copy, m0, m1):
+            dst = w_group[u][:].rearrange("p e m j -> p m j e")
+            engine_copy(out=dst[:, m0:m1], in_=w_cols[:, m0:m1, :, 2 * u : 2 * u + 2])
 
-        def quantise_w(u):
+        def quantise_w(u, e0, e1):
             nc.vector.quantize_mx(
-                out=w_code[u][:].bitcast(FP8X4), scales=w_scale[u][:], in_=w_group[u][:].rearrange("p e m j -> p (e m j)")
+                out=w_code[u][:, P * e0 : P * e1].bitcast(FP8X4),
+                scales=w_scale[u][:, P * e0 : P * e1],
+                in_=w_group[u][:, e0:e1].rearrange("p e m j -> p (e m j)"),
             )
 
-        for c in range(len(X_CHUNKS)):
-            quantise_x(c)
-        group_w(0, nc.scalar.copy)
-        quantise_w(0)
-        group_w(1, nc.vector.tensor_copy)
+        quantise_x(0)
+        group_w(0, nc.vector.tensor_copy, 0, W_SPLIT)
+        group_w(0, nc.scalar.copy, W_SPLIT, P)
+        group_w(1, nc.scalar.copy, 0, W_SPLIT_1)
+        quantise_w(0, 0, 1)
+        quantise_w(0, 1, 2)
+        quantise_x(1)
+        quantise_x(2)
+        group_w(1, nc.vector.tensor_copy, W_SPLIT_1, P)
 
         h = [keep.tile([P, S], F32, name="h%d" % t) for t in range(4)]
         h_rows = keep.tile([P, 4, S - V0], F32, name="h_rows")
 
-        def layer1(t, firsts, width):
+        def layer1(t, firsts, width, banks):
             w_cols_t = slice(P * (t % 2), P * (t % 2 + 1))
-            for first in firsts:
-                bank = psum.tile([P, width], F32, name="bank", tag="mx")
+            for first, b in zip(firsts, banks):
+                bank = psum.tile([P, width], F32, name="bank", tag="bank%d" % b)
                 nc.tensor.matmul_mx(
                     out=bank[:],
                     lhsT=w_code[t // 2][:, w_cols_t].bitcast(FP8X4),
                     lhsT_scale=w_scale[t // 2][:, w_cols_t],
-                    rhs=x_code[:, first : first + width].bitcast(FP8X4),
+                    rhs=x_code[first // HALF][:, first % HALF : first % HALF + width].bitcast(FP8X4),
                     rhs_scale=x_scale[:, first : first + width],
                     start=True,
                     stop=True,
                 )
-                if (t, first) == (0, QUARTER):
+                if t == 0 and first in (QUARTER, HALF):
                     nc.vector.tensor_scalar(out=h[t][:, first : first + width], in0=bank[:, 0:width], scalar1=0.0, scalar2=None, op0=ALU.max)
                 else:
                     nc.scalar.activation(out=h[t][:, first : first + width], in_=bank[:, 0:width], func=ACT.Relu)
@@ -147,7 +164,8 @@ def tile_picked_treeup_relu_e_kernel(tc, xT, w1, w2_words, w2_scales, share, off
         z_scale = [keep.tile([P, n], U8, name="z_scale%d" % c, align_bytes=64) for c, (s0, n) in enumerate(Z_CHUNKS)]
 
         def new_z(c):
-            z.setdefault(c, keep.tile([P, Z_CHUNKS[c][1], 4], BF16, name="z%d" % c, tag="z%d" % c, align_bytes=64))
+            tag = "z%d" % (1 if c == LAST_V else c)
+            z.setdefault(c, keep.tile([P, Z_CHUNKS[c][1], 4], BF16, name="z%d" % c, tag=tag, align_bytes=64))
 
         taken_pe = keep.tile([P, 4, V0], F32, name="taken_pe")
 
@@ -159,12 +177,21 @@ def tile_picked_treeup_relu_e_kernel(tc, xT, w1, w2_words, w2_scales, share, off
         def follow_pe(t, s0, n):
             follow(t, s0, n, taken_pe[:, t, s0 : s0 + n])
 
+        for v, (s0, n) in enumerate(V_CHUNKS):
+            taken.setdefault(v, keep.tile([P, 4, n], F32, name="taken%d" % v, align_bytes=64))
+
         def follow_v(v, t):
             s0, n = V_CHUNKS[v]
-            if t == 0:
-                tag = "taken0" if v == 0 else "turned1_1"
-                taken.setdefault(v, keep.tile([P, 4, n], F32, name="taken%d" % v, tag=tag, align_bytes=64))
             follow(t, s0, n, taken[v][:, t, :])
+
+        def follow_by_scalar(v):
+            s0, n = V_CHUNKS[v]
+            plain = keep.tile([P, 4, n], F32, name="plain", tag="w_group0", align_bytes=64)
+            for t in range(4):
+                nc.scalar.activation(out=plain[:, t, :], in_=h[t][:].indirect(offsets(par_sb, s0, n)), func=ACT.Copy)
+            nc.vector.tensor_tensor(
+                out=taken[v][:], in0=plain[:], in1=share_sb[:, s0 : s0 + n].unsqueeze(1).to_broadcast([P, 4, n]), op=ALU.mult
+            )
 
         def add(c):
             s0, n = Z_CHUNKS[c]
@@ -189,7 +216,7 @@ def tile_picked_treeup_relu_e_kernel(tc, xT, w1, w2_words, w2_scales, share, off
             first = own and e == 0
             last = not own and e == 1
             if first:
-                sums.setdefault((u, c), psum.tile([P, n // P, 2, P], F32, name="sum_bank", tag="mx"))
+                sums.setdefault((u, c), psum.tile([P, n // P, 2, P], F32, name="sum_bank", tag="bank%d" % SUM_BANKS[u][c]))
             bank = sums[(u, c)]
             for b in range(n // P):
                 nc.tensor.matmul(
@@ -208,7 +235,7 @@ def tile_picked_treeup_relu_e_kernel(tc, xT, w1, w2_words, w2_scales, share, off
 
         def turn_back(c):
             n = PE_CHUNKS[c][1]
-            bank = psum.tile([P, n // P, 2, P], F32, name="back_bank", tag="mx")
+            bank = psum.tile([P, n // P, 2, P], F32, name="back_bank", tag="bank%d" % BACK_BANKS[c])
             for u in range(2):
                 for b in range(n // P):
                     words = turned[c][u][:, b, :, :].rearrange("s p e -> s (p e)").bitcast(F32)
@@ -228,7 +255,7 @@ def tile_picked_treeup_relu_e_kernel(tc, xT, w1, w2_words, w2_scales, share, off
             s0, n = Z_CHUNKS[c]
             groups = [[0], [1]] if c == LAST_V else [[0, 1]]
             for group in groups:
-                bank = psum.tile([P, len(group), n], F32, name="obank", tag="mx")
+                bank = psum.tile([P, len(group), n], F32, name="obank", tag="bank%d" % (OUT_BANKS[c] + group[0]))
                 for m in group:
                     nc.tensor.matmul_mx(
                         out=bank[:, m - group[0], :],
@@ -239,7 +266,7 @@ def tile_picked_treeup_relu_e_kernel(tc, xT, w1, w2_words, w2_scales, share, off
                         start=True,
                         stop=True,
                     )
-                tag = "z%d" % LAST_V if c == LAST_PE else "res%d_%d" % (c, group[0])
+                tag = "z1" if c == LAST_PE else "res%d_%d" % (c, group[0])
                 res = keep.tile([P, len(group), n], F32, name="res%d_%d" % (c, group[0]), tag=tag, align_bytes=64)
                 dst = out.rearrange("(m p) s -> p m s", p=P)[:, group[0] : group[-1] + 1, s0 : s0 + n]
                 if group == [1] or c == LAST_PE:
@@ -252,12 +279,12 @@ def tile_picked_treeup_relu_e_kernel(tc, xT, w1, w2_words, w2_scales, share, off
                     nc.sync.dma_start(out=dst, in_=res[:])
 
         pe = range(len(PE_CHUNKS))
-        layer1(0, range(0, S, QUARTER), QUARTER)
-        quantise_w(1)
-        layer1(1, range(0, S, HALF), HALF)
-        for first, width in H_CHUNKS:
+        layer1(0, range(0, S, QUARTER), QUARTER, (0, 1, 2, 3))
+        quantise_w(1, 0, 2)
+        layer1(1, range(0, S, HALF), HALF, (1, 2))
+        for (first, width), banks in zip(H_CHUNKS, ((4, 5), (6, 7), (0, 3))):
             for t in (2, 3):
-                layer1(t, [first], width)
+                layer1(t, [first], width, [banks[t - 2]])
 
         for t in (0, 1):
             follow_pe(t, 0, V0)
@@ -268,6 +295,7 @@ def tile_picked_treeup_relu_e_kernel(tc, xT, w1, w2_words, w2_scales, share, off
         follow_v(0, 2)
         for a in range(0, V_CHUNKS[0][1], P):
             follow(3, V0 + a, P, taken[0][:, 3, a : a + P])
+        follow_by_scalar(1)
         for own, t in ((True, 0), (True, 1), (False, 0), (False, 1)):
             for c in pe:
                 turn(own, t, c)
@@ -282,10 +310,8 @@ def tile_picked_treeup_relu_e_kernel(tc, xT, w1, w2_words, w2_scales, share, off
         for c in (0, FIRST_V, 1):
             quantise_z(c)
             layer2(c)
-        for t in range(4):
-            follow_v(1, t)
-        quantise_z(LAST_PE)
         add(LAST_V)
+        quantise_z(LAST_PE)
         quantise_z(LAST_V)
         layer2(LAST_PE)
         layer2(LAST_V)

@@ -229,8 +229,8 @@ def tile_picked_treeup_relu_e_kernel(tc, xT, w1, w2_words, w2_scales, share, off
                 )
             if last:
                 nc.scalar.copy(
-                    out=turned[c][u][:].rearrange("s b (r i) e -> s b r e i", i=LINE),
-                    in_=bank[:].rearrange("s b e (r i) -> s b r e i", i=LINE),
+                    out=turned[c][u][:],
+                    in_=bank[:].rearrange("s b e p -> s b p e"),
                 )
 
         def turn_back(c):
@@ -241,8 +241,8 @@ def tile_picked_treeup_relu_e_kernel(tc, xT, w1, w2_words, w2_scales, share, off
                     words = turned[c][u][:, b, :, :].rearrange("s p e -> s (p e)").bitcast(F32)
                     nc.tensor.transpose(bank[:, b, u, :], words, ident[:])
             new_z(c)
-            z_words = z[c][:].rearrange("p n t -> p (n t)").bitcast(F32).rearrange("p (b r i u) -> p b r u i", u=2, i=LINE, r=P // LINE)
-            nc.scalar.copy(out=z_words, in_=bank[:].rearrange("p b u (r i) -> p b r u i", i=LINE))
+            z_words = z[c][:].rearrange("p n t -> p (n t)").bitcast(F32).rearrange("p (b s u) -> p b s u", u=2, s=P)
+            nc.scalar.copy(out=z_words, in_=bank[:].rearrange("p b u s -> p b s u"))
 
         def quantise_z(c):
             tag = "turned2_1" if c == FIRST_V else "z_code%d" % c

@@ -23,6 +23,7 @@ X_CHUNKS = [(0, 512), (512, 256), (768, 256)]
 W_SPLIT = 76
 W_SPLIT_1 = 96
 H_CHUNKS = [(0, 512), (512, 256), (768, 256)]
+V_RELU = [(0, 256), (0, 512)]
 QUARTER = S // 4
 HALF = S // 2
 PE_CHUNKS = [(0, 256), (256, 256), (512, 128)]
@@ -64,8 +65,9 @@ def tile_picked_treeup_relu_e_kernel(tc, xT, w1, w2_words, w2_scales, share, off
         w_raw = keep.tile([P, 4, H], F32, name="w_raw")
         nc.sync.dma_start(out=w_raw[:], in_=w1.rearrange("(p j) c -> p j c", j=4))
         nc.sync.dma_start(par_sb[:], par)
-        share_sb = keep.tile([P, S], F32, name="share_sb")
-        nc.sync.dma_start(out=share_sb[:], in_=share)
+        share_sb = [keep.tile([P, n], F32, name="share%d" % a, tag="share%d" % a, align_bytes=64) for a, n in enumerate((V0, HALF))]
+        nc.sync.dma_start(out=share_sb[0][:], in_=share[:, 0:V0])
+        nc.sync.dma_start(out=share_sb[1][:], in_=share[:, HALF:S])
         w2_code = keep.tile([P, 2 * N], U8, name="w2_code", align_bytes=64)
         nc.sync.dma_start(out=w2_code[:].bitcast(I32), in_=w2_words[0].bitcast(I32))
         for q in range(4):
@@ -151,7 +153,7 @@ def tile_picked_treeup_relu_e_kernel(tc, xT, w1, w2_words, w2_scales, share, off
                     start=True,
                     stop=True,
                 )
-                if t == 0 and first in (QUARTER, HALF):
+                if (t, first) in V_RELU:
                     nc.vector.tensor_scalar(out=h[t][:, first : first + width], in0=bank[:, 0:width], scalar1=0.0, scalar2=None, op0=ALU.max)
                 else:
                     nc.scalar.activation(out=h[t][:, first : first + width], in_=bank[:, 0:width], func=ACT.Relu)
@@ -164,33 +166,43 @@ def tile_picked_treeup_relu_e_kernel(tc, xT, w1, w2_words, w2_scales, share, off
         z_scale = [keep.tile([P, n], U8, name="z_scale%d" % c, align_bytes=64) for c, (s0, n) in enumerate(Z_CHUNKS)]
 
         def new_z(c):
-            tag = "z%d" % (1 if c == LAST_V else c)
+            tag = "turned1_1" if c == FIRST_V else "z%d" % (1 if c == LAST_V else c)
             z.setdefault(c, keep.tile([P, Z_CHUNKS[c][1], 4], BF16, name="z%d" % c, tag=tag, align_bytes=64))
 
         taken_pe = keep.tile([P, 4, V0], F32, name="taken_pe")
 
+        def shares(s0, n):
+            return share_sb[s0 // HALF][:, s0 % HALF : s0 % HALF + n]
+
         def follow(t, s0, n, dst):
             nc.vector.tensor_tensor(
-                out=dst, in0=h[t][:].indirect(offsets(par_sb, s0, n)), in1=share_sb[:, s0 : s0 + n], op=ALU.mult
+                out=dst, in0=h[t][:].indirect(offsets(par_sb, s0, n)), in1=shares(s0, n), op=ALU.mult
             )
 
         def follow_pe(t, s0, n):
             follow(t, s0, n, taken_pe[:, t, s0 : s0 + n])
 
-        for v, (s0, n) in enumerate(V_CHUNKS):
-            taken.setdefault(v, keep.tile([P, 4, n], F32, name="taken%d" % v, align_bytes=64))
+        def new_taken(v):
+            tag = ("share0", "taken1")[v]
+            taken.setdefault(v, keep.tile([P, 4, V_CHUNKS[v][1]], F32, name="taken%d" % v, tag=tag, align_bytes=64))
 
         def follow_v(v, t):
             s0, n = V_CHUNKS[v]
             follow(t, s0, n, taken[v][:, t, :])
 
-        def follow_by_scalar(v):
-            s0, n = V_CHUNKS[v]
-            plain = keep.tile([P, 4, n], F32, name="plain", tag="w_group0", align_bytes=64)
-            for t in range(4):
-                nc.scalar.activation(out=plain[:, t, :], in_=h[t][:].indirect(offsets(par_sb, s0, n)), func=ACT.Copy)
+        plain = {}
+
+        def fetch(t):
+            s0, n = V_CHUNKS[1]
+            if t == 0:
+                plain.setdefault(0, keep.tile([P, 4, n], F32, name="plain", tag="w_group0", align_bytes=64))
+            nc.scalar.activation(out=plain[0][:, t, :], in_=h[t][:].indirect(offsets(par_sb, s0, n)), func=ACT.Copy)
+
+        def weigh():
+            s0, n = V_CHUNKS[1]
+            new_taken(1)
             nc.vector.tensor_tensor(
-                out=taken[v][:], in0=plain[:], in1=share_sb[:, s0 : s0 + n].unsqueeze(1).to_broadcast([P, 4, n]), op=ALU.mult
+                out=taken[1][:], in0=plain[0][:], in1=shares(s0, n).unsqueeze(1).to_broadcast([P, 4, n]), op=ALU.mult
             )
 
         def add(c):
@@ -245,7 +257,7 @@ def tile_picked_treeup_relu_e_kernel(tc, xT, w1, w2_words, w2_scales, share, off
             nc.scalar.copy(out=z_words, in_=bank[:].rearrange("p b u s -> p b s u"))
 
         def quantise_z(c):
-            tag = "turned2_1" if c == FIRST_V else "z_code%d" % c
+            tag = "z_code%d" % c
             z_code.setdefault(c, keep.tile([P, Z_CHUNKS[c][1]], U32, name="z_code%d" % c, tag=tag, align_bytes=64))
             nc.vector.quantize_mx(
                 out=z_code[c][:].bitcast(FP8X4), scales=z_scale[c][:], in_=z[c][:].rearrange("p n t -> p (n t)")
@@ -266,10 +278,10 @@ def tile_picked_treeup_relu_e_kernel(tc, xT, w1, w2_words, w2_scales, share, off
                         start=True,
                         stop=True,
                     )
-                tag = "z1" if c == LAST_PE else "res%d_%d" % (c, group[0])
+                tag = "res%d_%d" % (c, group[0])
                 res = keep.tile([P, len(group), n], F32, name="res%d_%d" % (c, group[0]), tag=tag, align_bytes=64)
                 dst = out.rearrange("(m p) s -> p m s", p=P)[:, group[0] : group[-1] + 1, s0 : s0 + n]
-                if group == [1] or c == LAST_PE:
+                if group == [1]:
                     nc.vector.tensor_copy(out=res[:], in_=bank[:])
                 else:
                     nc.scalar.copy(out=res[:], in_=bank[:])
@@ -282,34 +294,46 @@ def tile_picked_treeup_relu_e_kernel(tc, xT, w1, w2_words, w2_scales, share, off
         layer1(0, range(0, S, QUARTER), QUARTER, (0, 1, 2, 3))
         quantise_w(1, 0, 2)
         layer1(1, range(0, S, HALF), HALF, (1, 2))
-        for (first, width), banks in zip(H_CHUNKS, ((4, 5), (6, 7), (0, 3))):
-            for t in (2, 3):
-                layer1(t, [first], width, [banks[t - 2]])
+        layer1(2, range(0, S, HALF), HALF, (4, 5))
+        layer1(3, range(0, S, HALF), HALF, (6, 7))
 
-        for t in (0, 1):
+        for t in (0, 1, 2):
             follow_pe(t, 0, V0)
-            follow_v(0, t)
         for s0, n in PE_CHUNKS:
-            follow_pe(2, s0, n)
             follow_pe(3, s0, n)
-        follow_v(0, 2)
-        for a in range(0, V_CHUNKS[0][1], P):
-            follow(3, V0 + a, P, taken[0][:, 3, a : a + P])
-        follow_by_scalar(1)
-        for own, t in ((True, 0), (True, 1), (False, 0), (False, 1)):
+        new_taken(0)
+        for t in range(4):
+            follow_v(0, t)
+        fetch(0)
+        fetch(1)
+        for own, t in ((True, 0), (True, 1), (False, 0)):
             for c in pe:
                 turn(own, t, c)
-        for c in pe:
+        for c in (0, 1):
+            turn(False, 1, c)
+
+        def second_pair(c):
             for own, t in ((True, 2), (True, 3), (False, 2), (False, 3)):
                 turn(own, t, c)
-            if c > 0:
-                turn_back(c - 1)
-        turn_back(LAST_PE)
 
+        second_pair(0)
+        turn(False, 1, 2)
+        fetch(2)
+        second_pair(1)
+        turn_back(0)
+        second_pair(2)
+        turn_back(1)
+        fetch(3)
+        turn_back(2)
+
+        quantise_z(0)
+        layer2(0)
+        quantise_z(1)
+        layer2(1)
         add(FIRST_V)
-        for c in (0, FIRST_V, 1):
-            quantise_z(c)
-            layer2(c)
+        weigh()
+        quantise_z(FIRST_V)
+        layer2(FIRST_V)
         add(LAST_V)
         quantise_z(LAST_PE)
         quantise_z(LAST_V)

@@ -23,7 +23,7 @@ X_CHUNKS = [(0, 512), (512, 256), (768, 256)]
 W_SPLIT = 76
 W_SPLIT_1 = 96
 H_CHUNKS = [(0, 512), (512, 256), (768, 256)]
-V_RELU = [(0, 256), (0, 512)]
+V_RELU = [(0, 512)]
 QUARTER = S // 4
 HALF = S // 2
 PE_CHUNKS = [(0, 256), (256, 256), (512, 128)]
@@ -33,9 +33,9 @@ V0 = V_CHUNKS[0][0]
 LAST_PE = len(PE_CHUNKS) - 1
 FIRST_V = len(PE_CHUNKS)
 LAST_V = len(Z_CHUNKS) - 1
-SUM_BANKS = [(1, 2, 4), (5, 6, 7)]
-BACK_BANKS = (0, 3, 1)
-OUT_BANKS = (2, 5, 6, 4, 0)
+SUM_BANKS = [(1, 2, 3), (4, 5, 6)]
+BACK_BANKS = (0, 7, 1)
+OUT_BANKS = (2, 4, 3, 5, 6)
 LINE = 4
 
 
@@ -65,9 +65,9 @@ def tile_picked_treeup_relu_e_kernel(tc, xT, w1, w2_words, w2_scales, share, off
         w_raw = keep.tile([P, 4, H], F32, name="w_raw")
         nc.sync.dma_start(out=w_raw[:], in_=w1.rearrange("(p j) c -> p j c", j=4))
         nc.sync.dma_start(par_sb[:], par)
-        share_sb = [keep.tile([P, n], F32, name="share%d" % a, tag="share%d" % a, align_bytes=64) for a, n in enumerate((V0, HALF))]
+        share_sb = [keep.tile([P, n], F32, name="share%d" % a, tag="share%d" % a, align_bytes=64) for a, n in enumerate((V0, S - QUARTER))]
         nc.sync.dma_start(out=share_sb[0][:], in_=share[:, 0:V0])
-        nc.sync.dma_start(out=share_sb[1][:], in_=share[:, HALF:S])
+        nc.sync.dma_start(out=share_sb[1][:], in_=share[:, QUARTER:S])
         w2_code = keep.tile([P, 2 * N], U8, name="w2_code", align_bytes=64)
         nc.sync.dma_start(out=w2_code[:].bitcast(I32), in_=w2_words[0].bitcast(I32))
         for q in range(4):
@@ -172,7 +172,7 @@ def tile_picked_treeup_relu_e_kernel(tc, xT, w1, w2_words, w2_scales, share, off
         taken_pe = keep.tile([P, 4, V0], F32, name="taken_pe")
 
         def shares(s0, n):
-            return share_sb[s0 // HALF][:, s0 % HALF : s0 % HALF + n]
+            return share_sb[0][:, 0:n] if s0 == 0 else share_sb[1][:, s0 - QUARTER : s0 - QUARTER + n]
 
         def follow(t, s0, n, dst):
             nc.vector.tensor_tensor(
@@ -194,15 +194,14 @@ def tile_picked_treeup_relu_e_kernel(tc, xT, w1, w2_words, w2_scales, share, off
 
         def fetch(t):
             s0, n = V_CHUNKS[1]
-            if t == 0:
-                plain.setdefault(0, keep.tile([P, 4, n], F32, name="plain", tag="w_group0", align_bytes=64))
-            nc.scalar.activation(out=plain[0][:, t, :], in_=h[t][:].indirect(offsets(par_sb, s0, n)), func=ACT.Copy)
+            if t == 1:
+                plain.setdefault(0, keep.tile([P, 3, n], F32, name="plain", tag="w_group0", align_bytes=64))
+            nc.scalar.activation(out=plain[0][:, t - 1, :], in_=h[t][:].indirect(offsets(par_sb, s0, n)), func=ACT.Copy)
 
         def weigh():
             s0, n = V_CHUNKS[1]
-            new_taken(1)
             nc.vector.tensor_tensor(
-                out=taken[1][:], in0=plain[0][:], in1=shares(s0, n).unsqueeze(1).to_broadcast([P, 4, n]), op=ALU.mult
+                out=taken[1][:, 1:4, :], in0=plain[0][:], in1=shares(s0, n).unsqueeze(1).to_broadcast([P, 3, n]), op=ALU.mult
             )
 
         def add(c):
@@ -294,18 +293,21 @@ def tile_picked_treeup_relu_e_kernel(tc, xT, w1, w2_words, w2_scales, share, off
         layer1(0, range(0, S, QUARTER), QUARTER, (0, 1, 2, 3))
         quantise_w(1, 0, 2)
         layer1(1, range(0, S, HALF), HALF, (1, 2))
-        layer1(2, range(0, S, HALF), HALF, (4, 5))
-        layer1(3, range(0, S, HALF), HALF, (6, 7))
+        layer1(2, range(0, S, HALF), HALF, (3, 1))
+        layer1(3, range(0, S, HALF), HALF, (2, 3))
 
         for t in (0, 1, 2):
             follow_pe(t, 0, V0)
+            if t == 0:
+                new_taken(1)
+                follow_v(1, 0)
         for s0, n in PE_CHUNKS:
             follow_pe(3, s0, n)
         new_taken(0)
         for t in range(4):
             follow_v(0, t)
-        fetch(0)
         fetch(1)
+        fetch(2)
         for own, t in ((True, 0), (True, 1), (False, 0)):
             for c in pe:
                 turn(own, t, c)
@@ -318,12 +320,11 @@ def tile_picked_treeup_relu_e_kernel(tc, xT, w1, w2_words, w2_scales, share, off
 
         second_pair(0)
         turn(False, 1, 2)
-        fetch(2)
+        fetch(3)
         second_pair(1)
         turn_back(0)
         second_pair(2)
         turn_back(1)
-        fetch(3)
         turn_back(2)
 
         quantise_z(0)

@@ -18,9 +18,9 @@ FP4X4 = mybir.dt.float4_e2m1fn_x4
 ALU = mybir.AluOpType
 ACT = mybir.ActivationFunctionType
 
-X_ROWS = {2: [(384, 256), (640, 128), (768, 256)], 3: [(512, 256), (768, 256)]}
+X_ROWS = {2: [(256, 256), (512, 256), (768, 256)], 3: [(512, 256), (768, 256)]}
 X_CHUNKS = [(0, 512), (512, 256), (768, 256)]
-W_SPLIT = 76
+W_SPLIT = 68
 W_SPLIT_1 = 96
 H_CHUNKS = [(0, 512), (512, 256), (768, 256)]
 V_RELU = [(0, 512)]

from contextlib import ExitStack

import concourse.mybir as mybir
from concourse.masks import make_identity

K, T, S, H, N = 512, 2048, 1024, 512, 256
P = 128
FLOPS = 2 * K * H * S + 2 * H * N * S

F32 = mybir.dt.float32
BF16 = mybir.dt.bfloat16
I32 = mybir.dt.int32
U32 = mybir.dt.uint32
U16 = mybir.dt.uint16
U8 = mybir.dt.uint8
FP8X4 = mybir.dt.float8_e4m3fn_x4
FP4X4 = mybir.dt.float4_e2m1fn_x4
ALU = mybir.AluOpType
ACT = mybir.ActivationFunctionType

X_ROWS = {2: [(256, 256), (512, 256), (768, 256)], 3: [(512, 256), (768, 256)]}
X_CHUNKS = [(0, 512), (512, 256), (768, 256)]
W_SPLIT = 68
W_SPLIT_1 = 96
H_CHUNKS = [(0, 512), (512, 256), (768, 256)]
V_RELU = [(0, 512)]
QUARTER = S // 4
HALF = S // 2
PE_CHUNKS = [(0, 256), (256, 256), (512, 128)]
V_CHUNKS = [(640, 256), (896, 128)]
Z_CHUNKS = PE_CHUNKS + V_CHUNKS
V0 = V_CHUNKS[0][0]
LAST_PE = len(PE_CHUNKS) - 1
FIRST_V = len(PE_CHUNKS)
LAST_V = len(Z_CHUNKS) - 1
SUM_BANKS = [(1, 2, 3), (4, 5, 6)]
BACK_BANKS = (0, 7, 1)
OUT_BANKS = (2, 4, 3, 5, 6)
LINE = 4


def tile_picked_treeup_relu_e_kernel(tc, xT, w1, w2_words, w2_scales, share, offs, par, out):
    nc = tc.nc
    with ExitStack() as ctx:
        keep = ctx.enter_context(tc.tile_pool(name="keep", bufs=1))
        psum = ctx.enter_context(tc.psum_pool(name="psum", bufs=1))

        offs_sb = keep.tile([P, S // 16], U16, name="offs_sb")
        par_sb = keep.tile([P, S // 16], U16, name="par_sb")
        w2_scale = keep.tile([P, N], U8, name="w2_scale", align_bytes=64)
        nc.gpsimd.memset(w2_scale[:], 0)
        ident = keep.tile([P, P], F32, name="ident")
        make_identity(nc, ident[:])
        warm_in = keep.tile([P, 1], F32, name="warm_in")
        warm_out = keep.tile([P, 1], F32, name="warm_out")
        nc.vector.memset(warm_in[:], 0.0)
        nc.scalar.activation(out=warm_out[:], in_=warm_in[:], func=ACT.Relu)

        x_rows = xT.rearrange("(p j) t -> p j t", j=4)
        raw = [keep.tile([P, T], F32, name="raw%d" % j) for j in range(4)]
        for j in range(4):
            nc.sync.dma_start(out=raw[j][:], in_=x_rows[:, j, :])
            if j == 0:
                nc.sync.dma_start(offs_sb[:], offs)
        w_raw = keep.tile([P, 4, H], F32, name="w_raw")
        nc.sync.dma_start(out=w_raw[:], in_=w1.rearrange("(p j) c -> p j c", j=4))
        nc.sync.dma_start(par_sb[:], par)
        share_sb = [keep.tile([P, n], F32, name="share%d" % a, tag="share%d" % a, align_bytes=64) for a, n in enumerate((V0, S - QUARTER))]
        nc.sync.dma_start(out=share_sb[0][:], in_=share[:, 0:V0])
        nc.sync.dma_start(out=share_sb[1][:], in_=share[:, QUARTER:S])
        w2_code = keep.tile([P, 2 * N], U8, name="w2_code", align_bytes=64)
        nc.sync.dma_start(out=w2_code[:].bitcast(I32), in_=w2_words[0].bitcast(I32))
        for q in range(4):
            nc.sync.dma_start(out=w2_scale[32 * q : 32 * q + 4, :].bitcast(I32), in_=w2_scales[0, 4 * q : 4 * q + 4, :].bitcast(I32))

        got = [keep.tile([P, 2, S], BF16, name="got%d" % u, tag="got%d" % u, align_bytes=64) for u in range(2)]
        picked = keep.tile([P, S, 4], BF16, name="picked", tag="picked", align_bytes=64)
        x_code = {}
        x_scale = keep.tile([P, S], U8, name="x_scale", align_bytes=64)

        def offsets(list_sb, s0, n):
            return list_sb[:, s0 // 16 : (s0 + n) // 16]

        def quantise_x(c):
            s0, n = X_CHUNKS[c]
            half, a = divmod(s0, HALF)
            if a == 0:
                x_code.setdefault(half, keep.tile([P, HALF], U32, name="x_code%d" % half, tag=("x_code0", "w_group0")[half], align_bytes=64))
            nc.vector.quantize_mx(
                out=x_code[half][:, a : a + n].bitcast(FP8X4),
                scales=x_scale[:, s0 : s0 + n],
                in_=picked[:, s0 : s0 + n, :].rearrange("p n j -> p (n j)"),
            )

        def pick_in_place(j, n):
            nc.vector.tensor_copy(out=picked[:, 0:n, j], in_=raw[j][:].indirect(offsets(offs_sb, 0, n)))

        def pick_row(j, s0, n):
            nc.scalar.activation(out=got[j // 2][:, j % 2, s0 : s0 + n], in_=raw[j][:].indirect(offsets(offs_sb, s0, n)), func=ACT.Copy)

        for j in (0, 1):
            pick_in_place(j, HALF)
            pick_row(j, HALF, HALF)
        nc.vector.tensor_copy(out=picked[:, HALF:S, 0:2], in_=got[0][:, :, HALF:S].rearrange("p e n -> p n e"))
        for j, pieces in X_ROWS.items():
            pick_in_place(j, pieces[0][0])
            for s0, n in pieces:
                pick_row(j, s0, n)
                if s0 + n < S:
                    nc.vector.tensor_copy(out=picked[:, s0 : s0 + n, j], in_=got[1][:, j % 2, s0 : s0 + n])
        s0 = S - QUARTER
        nc.scalar.copy(out=picked[:, s0:S, 2:4], in_=got[1][:, :, s0:S].rearrange("p e n -> p n e"))

        w_group = [keep.tile([P, 2, P, 4], BF16, name="w_group%d" % u, tag="w_group%d" % u, align_bytes=64) for u in range(2)]
        w_code = [keep.tile([P, 2 * P], U32, name="w_code%d" % u, tag=("w_code0", "picked")[u], align_bytes=64) for u in range(2)]
        w_scale = [keep.tile([P, 2 * P], U8, name="w_scale%d" % u, align_bytes=64) for u in range(2)]
        w_cols = w_raw[:].rearrange("p j (m t) -> p m j t", t=4)

        def group_w(u, engine_copy, m0, m1):
            dst = w_group[u][:].rearrange("p e m j -> p m j e")
            engine_copy(out=dst[:, m0:m1], in_=w_cols[:, m0:m1, :, 2 * u : 2 * u + 2])

        def quantise_w(u, e0, e1):
            nc.vector.quantize_mx(
                out=w_code[u][:, P * e0 : P * e1].bitcast(FP8X4),
                scales=w_scale[u][:, P * e0 : P * e1],
                in_=w_group[u][:, e0:e1].rearrange("p e m j -> p (e m j)"),
            )

        quantise_x(0)
        group_w(0, nc.vector.tensor_copy, 0, W_SPLIT)
        group_w(0, nc.scalar.copy, W_SPLIT, P)
        group_w(1, nc.scalar.copy, 0, W_SPLIT_1)
        quantise_w(0, 0, 1)
        quantise_w(0, 1, 2)
        quantise_x(1)
        quantise_x(2)
        group_w(1, nc.vector.tensor_copy, W_SPLIT_1, P)

        h = [keep.tile([P, S], F32, name="h%d" % t) for t in range(4)]
        h_rows = keep.tile([P, 4, S - V0], F32, name="h_rows")

        def layer1(t, firsts, width, banks):
            w_cols_t = slice(P * (t % 2), P * (t % 2 + 1))
            for first, b in zip(firsts, banks):
                bank = psum.tile([P, width], F32, name="bank", tag="bank%d" % b)
                nc.tensor.matmul_mx(
                    out=bank[:],
                    lhsT=w_code[t // 2][:, w_cols_t].bitcast(FP8X4),
                    lhsT_scale=w_scale[t // 2][:, w_cols_t],
                    rhs=x_code[first // HALF][:, first % HALF : first % HALF + width].bitcast(FP8X4),
                    rhs_scale=x_scale[:, first : first + width],
                    start=True,
                    stop=True,
                )
                if (t, first) in V_RELU:
                    nc.vector.tensor_scalar(out=h[t][:, first : first + width], in0=bank[:, 0:width], scalar1=0.0, scalar2=None, op0=ALU.max)
                else:
                    nc.scalar.activation(out=h[t][:, first : first + width], in_=bank[:, 0:width], func=ACT.Relu)
            if first + width == S:
                nc.sync.dma_start(out=h_rows[:, t, :], in_=h[t][:, V0:S])

        taken = {}
        z = {}
        z_code = {}
        z_scale = [keep.tile([P, n], U8, name="z_scale%d" % c, align_bytes=64) for c, (s0, n) in enumerate(Z_CHUNKS)]

        def new_z(c):
            tag = "turned1_1" if c == FIRST_V else "z%d" % (1 if c == LAST_V else c)
            z.setdefault(c, keep.tile([P, Z_CHUNKS[c][1], 4], BF16, name="z%d" % c, tag=tag, align_bytes=64))

        taken_pe = keep.tile([P, 4, V0], F32, name="taken_pe")

        def shares(s0, n):
            return share_sb[0][:, 0:n] if s0 == 0 else share_sb[1][:, s0 - QUARTER : s0 - QUARTER + n]

        def follow(t, s0, n, dst):
            nc.vector.tensor_tensor(
                out=dst, in0=h[t][:].indirect(offsets(par_sb, s0, n)), in1=shares(s0, n), op=ALU.mult
            )

        def follow_pe(t, s0, n):
            follow(t, s0, n, taken_pe[:, t, s0 : s0 + n])

        def new_taken(v):
            tag = ("share0", "taken1")[v]
            taken.setdefault(v, keep.tile([P, 4, V_CHUNKS[v][1]], F32, name="taken%d" % v, tag=tag, align_bytes=64))

        def follow_v(v, t):
            s0, n = V_CHUNKS[v]
            follow(t, s0, n, taken[v][:, t, :])

        plain = {}

        def fetch(t):
            s0, n = V_CHUNKS[1]
            if t == 1:
                plain.setdefault(0, keep.tile([P, 3, n], F32, name="plain", tag="w_group0", align_bytes=64))
            nc.scalar.activation(out=plain[0][:, t - 1, :], in_=h[t][:].indirect(offsets(par_sb, s0, n)), func=ACT.Copy)

        def weigh():
            s0, n = V_CHUNKS[1]
            nc.vector.tensor_tensor(
                out=taken[1][:, 1:4, :], in0=plain[0][:], in1=shares(s0, n).unsqueeze(1).to_broadcast([P, 3, n]), op=ALU.mult
            )

        def add(c):
            s0, n = Z_CHUNKS[c]
            new_z(c)
            for a in range(0, n, P):
                nc.vector.tensor_tensor(
                    out=z[c][:, a : a + P, :].rearrange("p (r i) t -> p r t i", i=LINE),
                    in0=taken[c - FIRST_V][:, :, a : a + P].rearrange("p t (r i) -> p r t i", i=LINE),
                    in1=h_rows[:, :, s0 - V0 + a : s0 - V0 + a + P].rearrange("p t (r i) -> p r t i", i=LINE),
                    op=ALU.add,
                )

        turned = [
            [keep.tile([P, n // P, P, 2], BF16, name="turned%d_%d" % (c, u), tag="turned%d_%d" % (c, u), align_bytes=64) for u in range(2)]
            for c, (s0, n) in enumerate(PE_CHUNKS)
        ]
        sums = {}

        def turn(own, t, c):
            s0, n = PE_CHUNKS[c]
            u, e = divmod(t, 2)
            first = own and e == 0
            last = not own and e == 1
            if first:
                sums.setdefault((u, c), psum.tile([P, n // P, 2, P], F32, name="sum_bank", tag="bank%d" % SUM_BANKS[u][c]))
            bank = sums[(u, c)]
            for b in range(n // P):
                nc.tensor.matmul(
                    bank[:, b, e, :],
                    lhsT=h[t][:, s0 + P * b : s0 + P * (b + 1)] if own else taken_pe[:, t, s0 + P * b : s0 + P * (b + 1)],
                    rhs=ident[:],
                    is_transpose=True,
                    start=first and b == 0,
                    stop=last and b == n // P - 1,
                )
            if last:
                nc.scalar.copy(
                    out=turned[c][u][:],
                    in_=bank[:].rearrange("s b e p -> s b p e"),
                )

        def turn_back(c):
            n = PE_CHUNKS[c][1]
            bank = psum.tile([P, n // P, 2, P], F32, name="back_bank", tag="bank%d" % BACK_BANKS[c])
            for u in range(2):
                for b in range(n // P):
                    words = turned[c][u][:, b, :, :].rearrange("s p e -> s (p e)").bitcast(F32)
                    nc.tensor.transpose(bank[:, b, u, :], words, ident[:])
            new_z(c)
            z_words = z[c][:].rearrange("p n t -> p (n t)").bitcast(F32).rearrange("p (b s u) -> p b s u", u=2, s=P)
            nc.scalar.copy(out=z_words, in_=bank[:].rearrange("p b u s -> p b s u"))

        def quantise_z(c):
            tag = "z_code%d" % c
            z_code.setdefault(c, keep.tile([P, Z_CHUNKS[c][1]], U32, name="z_code%d" % c, tag=tag, align_bytes=64))
            nc.vector.quantize_mx(
                out=z_code[c][:].bitcast(FP8X4), scales=z_scale[c][:], in_=z[c][:].rearrange("p n t -> p (n t)")
            )

        def layer2(c):
            s0, n = Z_CHUNKS[c]
            groups = [[0], [1]] if c == LAST_V else [[0, 1]]
            for group in groups:
                bank = psum.tile([P, len(group), n], F32, name="obank", tag="bank%d" % (OUT_BANKS[c] + group[0]))
                for m in group:
                    nc.tensor.matmul_mx(
                        out=bank[:, m - group[0], :],
                        lhsT=w2_code[:, 2 * P * m : 2 * P * (m + 1)].bitcast(FP4X4),
                        lhsT_scale=w2_scale[:, P * m : P * (m + 1)],
                        rhs=z_code[c][:].bitcast(FP8X4),
                        rhs_scale=z_scale[c][:],
                        start=True,
                        stop=True,
                    )
                tag = "res%d_%d" % (c, group[0])
                res = keep.tile([P, len(group), n], F32, name="res%d_%d" % (c, group[0]), tag=tag, align_bytes=64)
                dst = out.rearrange("(m p) s -> p m s", p=P)[:, group[0] : group[-1] + 1, s0 : s0 + n]
                if group == [1]:
                    nc.vector.tensor_copy(out=res[:], in_=bank[:])
                else:
                    nc.scalar.copy(out=res[:], in_=bank[:])
                if group == [0]:
                    nc.scalar.dma_start(out=dst, in_=res[:])
                else:
                    nc.sync.dma_start(out=dst, in_=res[:])

        pe = range(len(PE_CHUNKS))
        layer1(0, range(0, S, QUARTER), QUARTER, (0, 1, 2, 3))
        quantise_w(1, 0, 2)
        layer1(1, range(0, S, HALF), HALF, (1, 2))
        layer1(2, range(0, S, HALF), HALF, (3, 1))
        layer1(3, range(0, S, HALF), HALF, (2, 3))

        for t in (0, 1, 2):
            follow_pe(t, 0, V0)
            if t == 0:
                new_taken(1)
                follow_v(1, 0)
        for s0, n in PE_CHUNKS:
            follow_pe(3, s0, n)
        new_taken(0)
        for t in range(4):
            follow_v(0, t)
        fetch(1)
        fetch(2)
        for own, t in ((True, 0), (True, 1), (False, 0)):
            for c in pe:
                turn(own, t, c)
        for c in (0, 1):
            turn(False, 1, c)

        def second_pair(c):
            for own, t in ((True, 2), (True, 3), (False, 2), (False, 3)):
                turn(own, t, c)

        second_pair(0)
        turn(False, 1, 2)
        fetch(3)
        second_pair(1)
        turn_back(0)
        second_pair(2)
        turn_back(1)
        turn_back(2)

        quantise_z(0)
        layer2(0)
        quantise_z(1)
        layer2(1)
        add(FIRST_V)
        weigh()
        quantise_z(FIRST_V)
        layer2(FIRST_V)
        add(LAST_V)
        quantise_z(LAST_PE)
        quantise_z(LAST_V)
        layer2(LAST_PE)
        layer2(LAST_V)
